import numpy as np, ml_dtypes
CORES = [1,5,17,21,33,37,49,53]
N = 8
BF = ml_dtypes.bfloat16
def gentries(a):
    return np.ascontiguousarray(a.reshape(8, 16, -1).transpose(0, 2, 1)).reshape(8, -1)
def gtable(e):
    e = np.asarray(e); return np.ascontiguousarray(e.reshape(8, -1, 16).transpose(0, 2, 1)).reshape(128, -1).astype(np.int32)
W, C, M, LO, SH, RO = 4096, 32, 128, 24, 4, 5
def parts(rng):
    return rng.integers(0, 256, (N, 8, 16, W)), rng.integers(0, W, (N, 8, C, M)), rng.integers(LO, M + 1, (N, 8, C)), rng.integers(1000, 1800, (N, 8, C))
def pack(bank, s, n, t):
    return {"bank": np.ascontiguousarray(bank.reshape(N, 128, W)).astype(np.float32).astype(BF), "arms": np.stack([gtable(a.transpose(0, 2, 1).reshape(8, -1)) for a in s]),
            "len0": np.stack([gtable(a) for a in n]), "th": np.stack([gtable(a) for a in t])}
def setup_inputs(rng):
    return pack(*parts(rng))
def setup_inputs_ties(rng):
    bank, s, n, t = parts(rng); pool = rng.integers(0, 256, (1, 8, 16, 3)); pool[:, 2, :, 0] = 0; pool[:, 2, :, 1:] = 255
    pick = rng.integers(0, 3, (N, 8, 1, W)); pick[0::2, 6] = 1
    pick[1::2, 6] = np.where(rng.random((N // 2, 1, W)) < 0.03, pick[1::2, 6], 1)
    bank = np.take_along_axis(np.repeat(pool, N, axis=0), pick, 3)
    far = np.add.reduce(np.abs(pool[0][:, :, :, None] - pool[0][:, :, None, :]), axis=1)
    i = rng.integers(0, 3, (N, 8, C)); j = rng.integers(0, 3, (N, 8, C))
    n[:, 4] = M; z = np.add.accumulate(s[:, 4], axis=2) & (W - 1); h = (((z * z) >> SH) + s[:, 4]) & (W - 1)
    c = np.arange(C); bank[:, 4] = pool[:, 4, :, :1]
    bank[np.arange(N)[:, None], 4, 0, h[:, c, M - 1 - c % 2]] = pool[0, 4, 0, 0] ^ 1
    return pack(bank, s, n, far[np.arange(8)[None, :, None], i, j] + rng.integers(0, 2, (N, 8, C)))
def setup_inputs_ends(rng):
    bank, s, n, t = parts(rng); e = rng.integers(0, W, (3, C))
    bank[:, 5] = bank[0, 5].copy(); bank[0::2, 7][:, :, e[1]] = 0; bank[1::2, 7][:, :, e[1]] = 255
    u = (rng.random((N, 16, C)) * rng.integers(1, 56, C)).astype(np.int64)
    bank[0::2, 6][:, :, e[2]] = u[0::2]; bank[1::2, 6][:, :, e[2]] = 255 - u[1::2]
    np.put_along_axis(s[:, 5], n[:, 5, :, None] - 1, e[0][None, :, None], 2)
    np.put_along_axis(s[:, 6], n[:, 6, :, None] - 1, e[2][None, :, None], 2)
    np.put_along_axis(s[:, 7], n[:, 7, :, None] - 1, e[1][None, :, None], 2)
    last = np.take_along_axis(s, n[..., None] - 1, 3)[..., 0]; end = np.take_along_axis(bank, last[:, :, None, :], 3)
    t = np.add.reduce(np.abs(end - np.roll(end, 1, axis=0)), axis=2) + rng.integers(0, 2, (N, 8, C))
    t[:, 0] = 0; t[:, 1] = 4081
    return pack(bank, s, n, t)
def setup_inputs_lengths(rng):
    bank, s, n, t = parts(rng)
    n[:, 0] = LO; n[:, 1] = M
    x = rng.integers(LO + 1, M - LO, C); n[:, 2] = x
    n[1::2, 2] = M - x + rng.integers(-1, 2, (N // 2, C)); t[:, 2] = 4081
    n[:, 3] = M // 2 + rng.integers(-1, 2, (N, C)); t[:, 3] = 0
    n[:, 4] = rng.choice(np.array([LO, LO + 1, M - 1, M]), (N, C)); t[:, 4] = rng.choice(np.array([0, 4081]), (N, C))
    return pack(bank, s, n, t)
def setup_inputs_codes(rng):
    bank, s, n, t = parts(rng)
    s[:, 0] = W - 1; n[:, 0] = np.maximum(n[:, 0], rng.integers(LO, M + 1, (N, C))); n[:, 0, :4] = M
    bank[:, 0] = rng.integers(128, 256, (N, 16, W)); t[:, 0] = rng.integers(500, 900, (N, C))
    z = (M * (W - 1) - 1) & (W - 1); bank[:, 0, :, (((z * z) >> SH) + W - 1) & (W - 1)] = 0
    s[:, 1] = 0; s[:, 2] = s[:, 2] & (W - 2); s[:, 3] = s[:, 3] | 1
    s[:, 4] = s[:, 4, :, :1].copy(); s[:, 6] = rng.choice(np.array([0, 1, W - 2, W - 1]), (N, C, M))
    s[:, 5, :, LO - 1:] = 0; n[:, 5] = M
    s[:, 7] = rng.integers(W - 16, W, (N, C, M)); bank[:, 7] = rng.integers(192, 256, (N, 16, W)); t[:, 7] = rng.integers(250, 450, (N, C))
    bank[:, 7][:, :, (((W - 1) * (W - 1) >> SH) + np.arange(W - 16, W)) & (W - 1)] = 0
    return pack(bank, s, n, t)
def setup_inputs_spread(rng):
    bank, s, n, t = parts(rng)
    bank = np.minimum((np.exp2(rng.integers(0, 9, (N, 8, 1, W))) * rng.random((N, 8, 16, W))).astype(np.int64), 255)
    s = (W * rng.random((N, 8, C, M)) ** rng.choice(np.array([1, 2, 5]), (N, 8, C, 1))).astype(np.int64)
    n = np.minimum(LO + ((M + 1 - LO) * rng.random((N, 8, C)) ** rng.choice(np.array([1, 3]), (N, 8, 1))).astype(np.int64), M)
    t = np.minimum(np.exp2(12 * rng.random((N, 8, C))).astype(np.int64), 4081)
    return pack(bank, s, n, t)
def check_inputs(d):
    bad = []; v = np.asarray(d["bank"]).astype(np.float32)
    if not np.all((v >= 0) & (v <= 255) & (v == np.floor(v))): bad.append("bank holds whole numbers from 0 to 255")
    for k, lo, hi in (("arms", 0, W - 1), ("len0", LO, M), ("th", 0, 4081)):
        if np.min(d[k]) < lo or np.max(d[k]) > hi: bad.append("range of " + k)
    return bad
def reference(bank, arms, len0, th):
    B = bank.astype(np.float32).astype(np.int32).reshape(N, 8, 16, W)
    S = np.stack([gentries(a) for a in arms]).astype(np.int64).reshape(N, 8, M, C).transpose(0, 1, 3, 2)
    n = np.stack([gentries(a) for a in len0]).astype(np.int64); T = np.stack([gentries(a) for a in th]).astype(np.int64)
    A = np.zeros((N, 8, C), np.int64); k = np.arange(M)
    for t in range(RO):
        d = 1 + t % (N - 1)
        last = np.take_along_axis(S, n[..., None] - 1, 3)[..., 0]
        E = np.take_along_axis(B, last[:, :, None, :], 3)
        near = np.add.reduce(np.abs(E - np.roll(E, d, axis=0)), axis=2) < T
        S2 = np.where(near[..., None], np.roll(S, d, axis=0), S); n2 = np.where(near, np.roll(n, d, axis=0), n)
        L = np.minimum(n + n2, M)
        back = np.clip((n + n2)[..., None] - 1 - k, 0, M - 1)
        Q = np.where(k < n[..., None], S, np.take_along_axis(S2, back, 3) ^ 1)
        Q = np.where(k < L[..., None], Q, 0)
        z = (np.add.accumulate(Q, axis=3) + A[..., None]) & (W - 1)
        h = (((z * z) >> SH) + Q) & (W - 1)
        R = np.take_along_axis(B, h.reshape(N, 8, 1, C * M), 3).reshape(N, 8, 16, C, M)
        D = np.add.reduce(np.abs(R[..., 1:] - R[..., :-1]), axis=2)
        ok = (k[1:] >= LO) & (k[1:] < L[..., None])
        b = 1 + np.argmax(np.where(ok, D, -1), axis=3)
        A = A + np.take_along_axis(np.add.reduce(R, axis=2), b[..., None], 3)[..., 0]
        S = np.where(k < b[..., None], Q, 0); n = b
    ys = np.stack([gtable(a.transpose(0, 2, 1).reshape(8, -1)) for a in S]).astype(np.float32)
    yn = np.stack([gtable(a) for a in n]).astype(np.float32); ya = np.stack([gtable(a) for a in A]).astype(np.float32)
    return {"ys": ys, "yn": yn, "ya": ya}

@@ -1,0 +1,489 @@
+import numpy as np
+from concourse.mybir import AluOpType, AxisListType, ActivationFunctionType
+
+RO, M, LO, W, NR = 5, 128, 24, 4096, 8
+CFG = {
+    "KC": [24, 76, 128],
+    "SG": [(24, 54, "a"), (54, 76, "v"), (76, 106, "a"), (106, 128, "v")],
+    "SX": [24, 76, 128],
+    "FG": [(0, 28, "a"), (28, 52, "v"), (52, 80, "v"), (80, 105, "v")],
+    "TL": [("row", 24, 51, 0, 0), ("row", 51, 75, 0, 0), ("sum", 24, 75, 0, 0), ("row", 75, 103, 0, 0), ("row", 103, 128, 0, 0), ("sum", 75, 128, 0, 0)],
+    "PEN": "a", "OWND": False,
+    "cyc": 1.04, "pe": 0.52, "gat": 1.5, "tt2": 1.0, "sem": 70.0, "issue": 600.0, "land": 2200.0, "fix": 60.0, "peu": 400,
+    "lag": 3000.0, "seed": 3, "tries": 800, "temp": 200.0,
+    "cases": [{}, {"cyc": 0.9, "pe": 0.45, "gat": 1.1, "sem": 50.0, "land": 1600.0},
+              {"cyc": 1.2, "pe": 0.6, "gat": 2.0, "sem": 100.0, "land": 3000.0, "tt2": 2.0}],
+}
+NCH = len(CFG["KC"]) - 1
+REG, OWN, STR, ZED, EM = 416, 80, 288, 416, 136
+F32, BF, F16, I32, U16 = "float32", "bfloat16", "float16", "int32", "uint16"
+SCRATCH = {
+    "bk": ("sbuf", [128, W], BF), "ar": ("sbuf", [128, 256], I32), "ln": ("sbuf", [128, 4], I32), "ti": ("sbuf", [128, 4], I32),
+    "win": ("sbuf", [128, REG * 2 * RO + 8], F32), "em": ("sbuf", [128, EM * 2 * RO], BF), "el": ("sbuf", [128, EM * 2 * RO], BF),
+    "thf": ("sbuf", [128, 2], F32), "par": ("sbuf", [128, 256], I32), "sgn": ("sbuf", [128, 256], F32),
+    "iot": ("sbuf", [128, 144], BF), "nio": ("sbuf", [128, 104], BF), "low": ("sbuf", [128, 104], BF),
+    "pmi": ("sbuf", [128, 128], BF), "blk": ("sbuf", [128, 128], BF), "bm": ("sbuf", [128, 128], BF),
+    "pid": ("sbuf", [128, 2], I32), "pc": ("sbuf", [128, 8], F32),
+    "idp": ("sbuf", [128, 128], BF), "idn": ("sbuf", [128, 128], BF), "idm": ("sbuf", [128, 128], BF), "idb": ("sbuf", [128, 128], BF),
+    "dcl": ("sbuf", [128, 2048], BF), "wp": ("sbuf", [128, 144], BF), "w2": ("sbuf", [128, 144], BF), "wn": ("sbuf", [128, 144], BF),
+    "dg": ("sbuf", [128, 16], F32), "fp": ("sbuf", [128, 16], BF), "fn": ("sbuf", [128, 16], BF), "cm": ("sbuf", [128, 128], F32),
+    "yo": ("sbuf", [128, 256], F32), "yl": ("sbuf", [128, 2], F32), "yb": ("sbuf", [128, 2], F32),
+}
+for _s in range(2):
+    for _n, _c, _d in (("va", 128, F32), ("vb", 128, F32), ("y0", 128, F32), ("xs", 128, F32), ("mq", 128, F32), ("rr", 128, F32),
+                       ("si", 128, I32), ("hi", 128, I32), ("ho", 106, U16), ("R", 1680, BF), ("AB", 1664, BF), ("G", 1664, F16),
+                       ("xm", 128, F16), ("mz", 128, F16), ("aa", 104, F16), ("uu", 104, F16), ("off", 104, U16), ("pen", 104, BF),
+                       ("sm", 16, F32), ("ai", 8, F32), ("oq", 2, U16), ("orr", 2, U16), ("l8", 8, U16), ("gq", 16, F32), ("gr", 16, BF)):
+        SCRATCH["%s%d" % (_n, _s)] = ("sbuf", [128, _c], _d)
+    SCRATCH["K%d" % _s] = ("psum", [128, 512], F32)
+    for _c in range(NCH):
+        SCRATCH["X%d%d" % (_s, _c)] = ("psum", [128, 512], F32)
+ND = 6 - 2 * NCH
+for _c in range(ND):
+    SCRATCH["D%d" % _c] = ("psum", [128, 512], F32)
+NDMA = 10
+SEMAPHORES = (["cv", "ca", "cp", "cg", "sent"] + ["d%d" % i for i in range(NDMA)]
+              + ["a%s%d%d" % (k, t, s) for k in "SE" for t in range(RO) for s in range(2)])
+A, ACT = AluOpType, ActivationFunctionType
+M12, M7 = 1.5 * 2.0 ** 35, 1.5 * 2.0 ** 30
+
+
+def V(name, lo=0, hi=None, step=1):
+    return (name, lo, SCRATCH[name][1][1] if hi is None else hi, step)
+
+
+def cols(v):
+    return len(range(v[1], v[2], v[3]))
+
+
+def build():
+    ops, cur = [], [0]
+    cyc = CFG["cyc"]
+
+    def add(eng, kind, args, reads, writes, cost, lat=0.0, after=()):
+        ops.append({"eng": eng, "kind": kind, "args": args, "r": [x for x in reads if isinstance(x, tuple)], "w": list(writes),
+                    "cost": cost, "lat": lat, "after": list(after), "s": cur[0], "succ": []})
+        return len(ops) - 1
+
+    def two(*vs):
+        return all(SCRATCH[v[0]][2] in (BF, F16, U16) for v in vs)
+
+    def vcost(n, f):
+        return max(64, n * f) * cyc
+
+    def ts(out, in0, s1, s2, op0, op1=None):
+        add("v", "ts", (out, in0, s1, s2, op0, op1), [in0, s1, s2], [out], vcost(cols(out), 0.5 if two(out, in0) else 1))
+
+    def tt(out, in0, in1, op):
+        ps = SCRATCH[in0[0]][0] == "psum" or SCRATCH[in1[0]][0] == "psum"
+        add("v", "tt", (out, in0, in1, op), [in0, in1], [out], vcost(cols(out), 1 if ps else CFG["tt2"] if two(out, in0, in1) else 2))
+
+    def cp(out, in0):
+        add("v", "cp", (out, in0), [in0], [out], vcost(cols(out), 0.5 if two(out, in0) else 1))
+
+    def red(out, in0, op, ab=False):
+        add("v", "red", (out, in0, op, ab), [in0], [out], vcost(cols(in0), 1))
+
+    def fill(out, c):
+        add("v", "fill", (out, c), [], [out], vcost(cols(out), 0.5 if two(out) else 1))
+
+    def act(out, in0, func, bias=0.0, scale=1.0):
+        add("a", "act", (out, in0, func, bias, scale), [in0, bias, scale], [out], CFG["fix"] + cols(out) * cyc)
+
+    def gat(eng, out, win, off, mask=None):
+        add(eng, "gat", (out, win, off, mask), [win, off, mask], [out], 60 + cols(out) * CFG["gat"] * cyc)
+
+    def mm(lst):
+        while lst:
+            k, c = 0, 0
+            while k < len(lst) and (c < CFG["peu"] or k % 2):
+                k, c = k + 1, c + max(64, cols(lst[k][2]))
+            add("p", "mm", lst[:k], [x[1] for x in lst[:k]] + [x[2] for x in lst[:k]], [x[0] for x in lst[:k]], c * CFG["pe"], 60.0)
+            lst = lst[k:]
+
+    def iota(out, pattern, base, ch):
+        add("g", "iota", (out, pattern, base, ch), [], [out], 130 + 2 * cols(out) * cyc)
+
+    def load(eng, out, name, lo, hi, lat):
+        add(eng, "load", (out, name, lo, hi), [], [out], 60.0, lat)
+
+    def send(kind, t, s, src, dst):
+        i = add("g", "send", (kind, t, s, src, dst), [src], [], CFG["issue"])
+        add(None, "arr", "a%s%d%d" % (kind, t, s), [], [dst], 0.0, CFG["land"] + (500 if kind == "S" else 0), after=[i])
+
+    load("s", V("ar"), "arms", 0, 256, 2200.0)
+    load("a", V("ln", 0, 2), "len0", 0, 2, 2000.0)
+    load("a", V("ti", 0, 2), "th", 0, 2, 2000.0)
+    load("s", V("bk", 0, 2048), "bank", 0, 2048, 5000.0)
+    load("a", V("bk", 2048, W), "bank", 2048, W, 5000.0)
+    iota(V("pid", 0, 1), [[0, 1]], 0, 1)
+    iota(V("iot"), [[1, 144]], 0, 0)
+    iota(V("pmi"), [[1, 128]], 0, -1)
+    iota(V("blk"), [[16, 8], [0, 16]], 0, 0)
+    ts(V("pid", 1, 2), V("pid", 0, 1), 15, None, A.bitwise_and)
+    CL, P16, P15, CLR = V("pc", 0, 1), V("pc", 1, 2), V("pc", 2, 3), V("pc", 3, 4)
+    cp(CL, V("pid", 1, 2))
+    ts(P16, V("pid", 0, 1), CL, None, A.subtract)
+    ts(P15, P16, 15.0, None, A.add)
+    ts(CLR, CL, -16.0 * (LO - 1), None, A.add)
+    ts(V("dg"), V("iot", 0, 16), CL, None, A.is_equal)
+    ts(V("bm"), V("blk"), P16, None, A.is_equal)
+    fill(V("cm"), -1.5)
+    fill(V("em", 129, EM * 2 * RO, EM), 0.0)
+    ts(V("fp"), V("iot", 0, 16), CL, None, A.is_equal)
+    ts(V("fn"), V("iot", 0, 16), CL, -1.0, A.is_equal, A.mult)
+    ts(V("nio"), V("iot", LO, M), -1.0, OWN - 1.0, A.mult, A.add)
+    ts(V("low"), V("iot", LO, M), -1.0, 75.5, A.mult, A.add)
+    for name, c in (("idp", 1.0), ("idn", -1.0), ("idm", 2.0 ** -9), ("idb", -2.0 ** 20)):
+        ts(V(name), V("pmi"), 0.0, c, A.is_equal, A.mult)
+    modes = [x[0] for x in CFG["TL"]]
+    for name, c in (("wp", 128.0),) + ((("w2", 256.0), ("wn", -128.0)) if "max" in modes else ()):
+        ts(V(name), V("iot"), P15, c, A.is_equal, A.mult)
+    ts(V("pmi"), V("pmi"), 0.0, -1.0 / 64, A.is_equal, A.mult)
+    for cl in range(16):
+        act(V("dcl", 128 * cl, 128 * cl + 128), V("pmi"), ACT.Copy, 0.0, V("dg", cl, cl + 1))
+    cp(V("thf"), V("ti", 0, 2))
+    ts(V("par"), V("ar"), 1, None, A.bitwise_and)
+    ts(V("sgn"), V("par"), -0.5, None, A.add)
+    fill(V("win", 0, OWN), 0.0)
+    for i in range(2 * RO):
+        fill(V("win", REG * i + OWN + M, REG * i + STR), 0.0)
+        fill(V("win", REG * (i + 1), min(REG * (i + 1) + OWN, REG * 2 * RO + 8)), 0.0)
+
+    def ends(t, s):
+        B = lambda n, lo=0, hi=None, st=1: V("%s%d" % (n, s), lo, hi, st)
+        e0 = EM * (2 * t + s)
+        gat("v", B("gq"), B("va"), B("oq", 0, 1), V("dg"))
+        red(B("sm", 2, 3), B("gq"), A.add)
+        ts(B("l8"), V("cm", 0, 8), B("sm", 2, 3), None, A.add)
+        gat("v", V("em", e0, e0 + 128), V("bk"), B("l8"), V("bm"))
+        send("E", t, s, V("em", e0, e0 + 130), V("el", e0, e0 + 130))
+
+    def gain(t, s):
+        K = "K%d" % s
+        mm([(V(K, 108, 109), V("wp", 15 - cl, 143 - cl), V("gr%d" % s, cl, cl + 1), cl == 0, cl == 15) for cl in range(16)])
+        act(V("ai%d" % s, t + 1, t + 2), V(K, 108, 109), ACT.Identity, V("ai%d" % s, t, t + 1), 1.0 / 128)
+
+    for s in range(2):
+        B = lambda n, lo=0, hi=None, st=1: V("%s%d" % (n, s), lo, hi, st)
+        w0, cur[0] = REG * s, s
+        ts(B("va"), V("ar", s, 256, 2), 1.5, None, A.add)
+        tt(B("y0"), B("va"), V("sgn", s, 256, 2), A.mult)
+        ts(V("win", w0 + OWN, w0 + OWN + M), B("y0"), -0.25, None, A.add)
+        send("S", 0, s, V("win", w0 + OWN, w0 + OWN + M), V("win", w0 + STR, w0 + STR + M))
+        act(B("xs"), V("win", w0 + OWN, w0 + OWN + M), ACT.Copy, 0.0, 1.0 / 64)
+        cp(V("em", EM * s + 128, EM * s + 129), V("ln", s, s + 1))
+        ts(B("oq", 0, 1), V("ln", s, s + 1), -1.0, None, A.add)
+        fill(B("ai", 0, 1), -2047.5)
+        ends(0, s)
+
+    KC = CFG["KC"]
+    tile = [0]
+    for t in range(RO):
+        for s in range(2):
+            B = lambda n, lo=0, hi=None, st=1: V("%s%d" % (n, s), lo, hi, st)
+            e0, w0, w1 = EM * (2 * t + s), REG * (2 * t + s), REG * (2 * t + 2 + s)
+            n_, n2 = V("em", e0 + 128, e0 + 129), V("el", e0 + 128, e0 + 129)
+            K, cur[0] = "K%d" % s, s
+            rng = [(0 if c == 0 else KC[c], KC[c + 1], "X%d%d" % (s, c)) for c in range(NCH)]
+            ts(B("mz"), V("iot", 0, M), n_, 512.0, A.is_lt, A.mult)
+            ts(B("aa"), V("nio"), n_, n_, A.add, A.add)
+            tt(B("uu"), B("aa"), B("mz", LO, M), A.add)
+            for lo, hi, X in rng:
+                tt(B("xm", lo, hi), B("xs", lo, hi) if t == 0 else V(X, lo, hi), B("mz", lo, hi), A.mult)
+            mm([(V(K, 112, 128), V("em", e0, e0 + 128), V("fp"), True, False), (V(K, 112, 128), V("el", e0, e0 + 128), V("fn"), False, True)])
+            ts(B("sm", 4, 5), n2, n_, float(STR - OWN), A.subtract, A.add)
+            red(B("sm", 3, 4), V(K, 112, 128), A.add, True)
+            ts(B("sm", 5, 6), B("sm", 3, 4), V("thf", s, s + 1), B("sm", 4, 5), A.is_lt, A.mult)
+            ts(B("off"), B("uu"), B("sm", 5, 6), float(ZED), A.add, A.min)
+            if t:
+                gain(t - 1, s)
+            for lo, hi, X in rng:
+                for a, b, eng in CFG["SG"]:
+                    if lo <= a < hi:
+                        gat(eng, B("G", 16 * (a - LO), 16 * (b - LO)), V("win", w0, w0 + REG + 8), B("off", a - LO, b - LO))
+                cuts = [k for k in CFG["SX"] if max(lo, LO) <= k <= hi]
+                mm([(V(X, lo, hi), V("idm"), B("xm", lo, hi), True, False)])
+                for a, b in zip(cuts, cuts[1:]):
+                    mm([(V(X, a, b), V("dcl", 128 * cl, 128 * cl + 128), B("G", 16 * (a - LO) + cl, 16 * (b - LO), 16), False,
+                         cl == 15 and b == cuts[-1]) for cl in range(16)])
+            for c, (lo, hi, X) in enumerate(rng):
+                hl = max(lo, LO - 1)
+                act(B("va", lo, hi), V(X, lo, hi), ACT.Abs, 0.5, 128.0)
+                ini = B("ai", t, t + 1) if c == 0 else B("sm", 8 + c, 9 + c)
+                add("v", "scan", (V(X, 128 + lo, 128 + hi), V("cm", lo, hi), B("va", lo, hi), ini),
+                    [V("cm", lo, hi), B("va", lo, hi), ini], [V(X, 128 + lo, 128 + hi)], vcost(hi - lo, 1))
+                ts(B("mq", hl, hi), V(X, 128 + hl, 128 + hi), M12, M12, A.add, A.subtract)
+                tt(B("rr", hl, hi), V(X, 128 + hl, 128 + hi), B("mq", hl, hi), A.subtract)
+                if c + 1 < NCH:
+                    cp(B("sm", 9 + c, 10 + c), V(X, 127 + hi, 128 + hi))
+                act(B("vb", hl, hi), B("va", hl, hi), ACT.Identity, -1.75)
+                act(V(X, 256 + hl, 256 + hi), B("rr", hl, hi), ACT.Square, 511.875, 0.25)
+                tt(B("si", hl, hi), V(X, 256 + hl, 256 + hi), B("vb", hl, hi), A.add)
+                ts(B("hi", hl, hi), B("si", hl, hi), W - 1, None, A.bitwise_and)
+                cp(B("ho", hl - LO + 1, hi - LO + 1), B("hi", hl, hi))
+                if t + 1 < RO:
+                    act(V("win", w1 + OWN + lo, w1 + OWN + hi), V(X, lo, hi), ACT.Copy, 0.0, 64.0)
+            if t + 1 < RO:
+                send("S", t + 1, s, V("win", w1 + OWN, w1 + OWN + M), V("win", w1 + STR, w1 + STR + M))
+            else:
+                act(B("y0"), B("va"), ACT.Identity, -1.5)
+            if CFG["PEN"] == "a":
+                act(B("pen"), B("va", LO, M), ACT.Relu, 1.5, -1.0)
+            else:
+                ts(B("pen"), B("va", LO, M), 0.5, None, A.is_equal)
+            mm([(V(K, 0, 104), V("idp"), V("low"), True, False), (V(K, 0, 104), V("idb"), B("pen"), False, False)])
+            for a, b, eng in CFG["FG"]:
+                gat(eng, B("R", 16 * a, 16 * b), V("bk"), B("ho", a, b))
+            TL, at = CFG["TL"], 0
+            for ti, (mode, a, b, c0, c1) in enumerate(TL):
+                j0, j1, o, wd, fin = 16 * (a - LO), 16 * (b - LO), V(K, a - LO, b - LO), b - a, ti + 1 == len(TL)
+                sel = lambda n, cl: V(n, 15 - cl, 143 - cl)
+                if mode in ("abs", "row"):
+                    D = "D%d" % (s * (ND // 2) + tile[0] % (ND // 2) if CFG["OWND"] else tile[0] % ND)
+                    tile[0] += 1
+                if mode == "max":
+                    tt(B("AB", at, at + 16 * wd), B("R", j0 + 16, j1 + 16), B("R", j0, j1), A.max)
+                    mm([(o, sel("wn", cl), B("R", j0 + u + cl, j1 + u, 16), False, False) for cl in range(16) for u in (0, 16)])
+                    mm([(o, sel("w2", cl), B("AB", at + cl, at + 16 * wd, 16), False, fin and cl == 15) for cl in range(16)])
+                    at += 16 * wd
+                elif mode == "abs":
+                    mm([(V(D, (cl - c0) * wd, (cl - c0 + 1) * wd), V(nm), B("R", j0 + u + cl, j1 + u, 16), u == 16, u == 0)
+                        for cl in range(c0, c1) for nm, u in (("idp", 16), ("idn", 0))])
+                    act(B("AB", at, at + (c1 - c0) * wd), V(D, 0, (c1 - c0) * wd), ACT.Abs)
+                    mm([(o, sel("wp", cl), B("AB", at + (cl - c0) * wd, at + (cl - c0 + 1) * wd), False, fin and cl == c1 - 1) for cl in range(c0, c1)])
+                    at += (c1 - c0) * wd
+                elif mode == "row":
+                    mm([(V(D, 0, j1 - j0), V("idp"), B("R", j0 + 16, j1 + 16), True, False), (V(D, 0, j1 - j0), V("idn"), B("R", j0, j1), False, True)])
+                    act(B("AB", at, at + 16 * wd), V(D, 0, j1 - j0), ACT.Abs)
+                    at += 16 * wd
+                else:
+                    mm([(o, sel("wp", cl), B("AB", at - 16 * wd + cl, at, 16), False, fin and cl == 15) for cl in range(16)])
+            m_, q_ = B("sm", 0, 1), B("sm", 1, 2)
+            red(m_, V(K, 0, 104), A.max)
+            ts(q_, m_, M7, M7, A.add, A.subtract)
+            if t + 1 < RO:
+                nn = V("em", e0 + 2 * EM + 128, e0 + 2 * EM + 129)
+                ts(B("oq", 0, 1), q_, m_, 74.5, A.subtract, A.add)
+                ts(nn, q_, m_, 75.5, A.subtract, A.add)
+                ends(t + 1, s)
+            else:
+                nn = V("yl", s, s + 1)
+                ts(nn, q_, m_, 75.5, A.subtract, A.add)
+                ts(B("mz"), V("iot", 0, M), nn, None, A.is_lt)
+                tt(V("yo", s, 256, 2), B("y0"), B("mz"), A.mult)
+            ts(B("orr", 0, 1), nn, 16.0, CLR, A.mult, A.add)
+            gat("a", B("gr"), B("R"), B("orr", 0, 1))
+            if t + 1 == RO:
+                gain(t, s)
+                act(V("yb", s, s + 1), B("ai", t + 1, t + 2), ACT.Identity, 2047.5)
+    add("s", "store", ("ys", V("yo")), [V("yo")], [], 60.0, 2200.0)
+    add("s", "store", ("yn", V("yl")), [V("yl")], [], 60.0, 2000.0)
+    add("a", "store", ("ya", V("yb")), [V("yb")], [], 60.0, 2000.0)
+    return ops
+
+
+def link(ops):
+    hist = {}
+    for i, o in enumerate(ops):
+        deps = dict((j, False) for j in o["after"])
+        acc = [(v, False) for v in o["r"]] + [(v, True) for v in o["w"]]
+        for v, wr in acc:
+            ps = SCRATCH[v[0]][0] == "psum"
+            for j, lo, hi, w in hist.get(v[0], ()):
+                same = ops[j]["eng"] == o["eng"] and ops[j]["kind"] not in ("load", "send") and o["kind"] not in ("store", "send")
+                hit = lo < v[2] and v[1] < hi
+                if ps:
+                    need = (not same) or (hit and w and not wr)
+                elif hit and (w or wr):
+                    need = True
+                else:
+                    continue
+                if o["eng"] == "p" and same:
+                    need = False
+                deps[j] = deps.get(j, False) or need
+        o["deps"] = deps
+        for j in deps:
+            ops[j]["succ"].append(i)
+        for v, wr in acc:
+            h = hist.setdefault(v[0], [])
+            if SCRATCH[v[0]][0] == "psum":
+                h[:] = [x for x in h[-24:] if x[0] != i or (x[3] and not wr)]
+                v = (v[0], 0, 512) if o["eng"] == "p" else v
+            elif wr and v[3] == 1:
+                h[:] = [x for x in h if not (v[1] <= x[1] and x[2] <= v[2])]
+            h.append((i, v[1], v[2], wr))
+
+
+def order(ops, bias):
+    n = len(ops)
+    sem = CFG["sem"]
+    prio = [0.0] * n
+    for i in range(n - 1, -1, -1):
+        prio[i] = ops[i]["cost"] + ops[i]["lat"] + max([prio[k] + (sem if ops[k]["deps"][i] else 0) for k in ops[i]["succ"]], default=0.0)
+    heap = [(-prio[i] - bias[i], i) for i in range(n) if not ops[i]["deps"]]
+    left = [len(o["deps"]) for o in ops]
+    busy, out, end, start = {}, [], [0.0] * n, [0.0] * n
+    while heap:
+        heap.sort()
+        i = heap.pop(0)[1]
+        o = ops[i]
+        at = max([end[j] + sem if w else end[j] if not o["eng"] else start[j] + ops[j]["cost"] for j, w in o["deps"].items()], default=0.0)
+        if o["eng"]:
+            lst = busy.setdefault(o["eng"], [])
+            p = len(lst)
+            while p and lst[p - 1][1] > at:
+                p -= 1
+            while p < len(lst) and at + o["cost"] > lst[p][0]:
+                at = max(at, lst[p][1])
+                p += 1
+            lst.insert(p, (at, at + o["cost"]))
+        start[i], end[i] = at, at + o["cost"] + o["lat"]
+        out.append(i)
+        for k in o["succ"]:
+            left[k] -= 1
+            if not left[k]:
+                heap.append((-prio[k] - bias[k], k))
+    pos = dict((i, p) for p, i in enumerate(out))
+    return sorted(out, key=lambda i: (start[i], pos[i])), start, end
+
+
+def replay(ops, seq, case):
+    cost, lat, sem = case
+    free, end = {}, [0.0] * len(ops)
+    for i in seq:
+        e = ops[i]["eng"]
+        at = max([free.get(e, 0.0)] + [end[j] + sem if w else end[j] for j, w in ops[i]["deps"].items() if w or not e])
+        if e:
+            free[e] = at + cost[i]
+        end[i] = at + cost[i] + lat[i]
+    return max(end)
+
+
+PLAN = []
+
+
+def plan():
+    if not PLAN:
+        cases, keep = [], dict(CFG)
+        for c in CFG["cases"]:
+            CFG.update(c)
+            ops = build()
+            cases.append(([o["cost"] for o in ops], [o["lat"] for o in ops], CFG["sem"]))
+            CFG.update(keep)
+        ops = build()
+        link(ops)
+        rs = np.random.RandomState(CFG["seed"])
+        bias = [-CFG["lag"] * o["s"] for o in ops]
+        for i, o in enumerate(ops):
+            if o["kind"] == "load":
+                bias[i] = 1e6 * (20 - i)
+        per = [i for i, o in enumerate(ops) if o["kind"] == "scan"]
+        per = per[NCH] - per[0]
+        now, best = 1e30, None
+        for it in range(CFG["tries"] + 1):
+            b2 = list(bias)
+            at, wide, step = int(rs.randint(5, len(ops))), int(rs.choice([1, 2, 4, 8, 16, 40])), int(rs.choice([len(ops), 2 * per, per]))
+            amount = float(rs.normal()) * float(rs.choice([300.0, 1000.0, 3000.0])) * (it > 0)
+            for j in range(at % step, len(ops), step):
+                for i in range(j, min(j + wide, len(ops))):
+                    b2[i] += amount
+            got = order(ops, b2)
+            all_ = [replay(ops, got[0], c) for c in cases]
+            val = sum(all_) / len(all_)
+            if val <= now + CFG["temp"] * (1 - it / (CFG["tries"] + 1)) * float(rs.exponential()):
+                now, bias = val, b2
+                if best is None or now < best[3]:
+                    best = got + (val, all_)
+        PLAN.append((ops,) + best)
+    return PLAN[0]
+
+
+def rank_program(g, core, T, topo):
+    rank = T.rank_of(core)
+    if rank is None:
+        return
+    ops, seq = plan()[:2]
+    peers = [T.cores[(rank + 1 + t % (NR - 1)) % NR] for t in range(RO)]
+    mask = -1
+    for a in T.cores:
+        for b in T.cores:
+            if a != b:
+                mask &= topo.mask(a, b)
+    lanes = bin(mask).count("1")
+    queue = {"v": g.vector, "a": g.scalar, "p": g.tensor, "g": g, "s": g.sync}
+    csem = {"v": "cv", "a": "ca", "p": "cp", "g": "cg"}
+    total, known, mark, clock = {}, dict((e, {}) for e in queue), {}, {}
+
+    def ap(v):
+        if not isinstance(v, tuple):
+            return v
+        return T[v[0]][:, v[1]:v[2]] if v[3] == 1 else T[v[0]][:, v[1]:v[2]:v[3]]
+
+    ndma = 0
+    for i in seq:
+        o = ops[i]
+        e, kind, x = o["eng"], o["kind"], o["args"]
+        if kind == "arr":
+            mark[i], clock[i], total[x] = (x, lanes), {}, lanes
+            continue
+        q, kn = queue[e], known[e]
+        need = sorted([j for j, w in o["deps"].items() if w and j in mark], key=lambda j: -mark[j][1])
+        for j in need:
+            sname, cnt = mark[j]
+            if kn.get(sname, 0) < cnt:
+                q.wait_ge(T.sem[sname], cnt)
+                kn[sname] = cnt
+                for k2, c2 in clock[j].items():
+                    kn[k2] = max(kn.get(k2, 0), c2)
+        clock[i] = dict(kn)
+        if kind == "send":
+            rid, pid = topo.addr(peers[x[1]])[:2]
+            g.remote_dma(ap(x[4]), ap(x[3]), T.sem["a%s%d%d" % x[:3]], T.sem.sent, pid, rid, mask)
+            total["sent"] = total.get("sent", 0) + lanes
+            continue
+        if kind in ("load", "store"):
+            sname = "d%d" % ndma
+            ndma += 1
+            ins = q.dma_start(ap(x[0]), T[x[1]][:, x[2]:x[3]]) if kind == "load" else q.dma_start(T[x[0]][:], ap(x[1]))
+            ins.then_inc(T.sem[sname], 16)
+            mark[i], total[sname] = (sname, 16), 16
+            continue
+        if kind == "ts":
+            ins = (q.tensor_scalar(ap(x[0]), ap(x[1]), ap(x[2]), None, x[4]) if x[5] is None
+                   else q.tensor_scalar(ap(x[0]), ap(x[1]), ap(x[2]), ap(x[3]), x[4], x[5]))
+        elif kind == "tt":
+            ins = q.tensor_tensor(ap(x[0]), ap(x[1]), ap(x[2]), x[3])
+        elif kind == "cp":
+            ins = q.tensor_copy(ap(x[0]), ap(x[1]))
+        elif kind == "red":
+            ins = q.tensor_reduce(ap(x[0]), ap(x[1]), AxisListType.X, x[2], apply_absolute_value=x[3])
+        elif kind == "fill":
+            ins = q.memset(ap(x[0]), x[1])
+        elif kind == "scan":
+            ins = q.tensor_tensor_scan(ap(x[0]), ap(x[1]), ap(x[2]), ap(x[3]), A.add, A.add)
+        elif kind == "act":
+            ins = q.activation(ap(x[0]), ap(x[1]), x[2], bias=ap(x[3]), scale=ap(x[4]))
+        elif kind == "gat":
+            src = ap(x[1]).indirect(ap(x[2]))
+            if e == "a":
+                ins = q.activation(ap(x[0]), src, ACT.Copy)
+            elif x[3] is None:
+                ins = q.tensor_copy(ap(x[0]), src)
+            else:
+                ins = q.tensor_tensor(ap(x[0]), src, ap(x[3]), A.mult)
+        elif kind == "iota":
+            if SCRATCH[x[0][0]][2] == I32:
+                ins = q.iota(ap(x[0]), x[1], x[2], x[3])
+            else:
+                ins = q.iota(ap(x[0]), x[1], x[2], x[3], allow_small_or_imprecise_dtypes=True)
+        else:
+            for mo, ml, mr, st, sp in x:
+                ins = q.matmul(ap(mo), ap(ml), ap(mr), st, sp)
+        sname = csem[e]
+        total[sname] = total.get(sname, 0) + 1
+        ins.then_inc(T.sem[sname], 1)
+        mark[i] = (sname, total[sname])
+    for sname, cnt in total.items():
+        if known["s"].get(sname, 0) < cnt:
+            g.sync.wait_ge(T.sem[sname], cnt)

@@ -3,37 +3,31 @@ from concourse.mybir import AluOpType, AxisListType, ActivationFunctionType
 
 RO, M, LO, W, NR = 5, 128, 24, 4096, 8
 CFG = {
-    "KC": [24, 76, 128],
-    "SG": [(24, 54, "a"), (54, 76, "v"), (76, 106, "a"), (106, 128, "v")],
-    "SX": [24, 76, 128],
-    "FG": [(0, 28, "a"), (28, 52, "v"), (52, 80, "v"), (80, 105, "v")],
-    "TL": [("row", 24, 51, 0, 0), ("row", 51, 75, 0, 0), ("sum", 24, 75, 0, 0), ("row", 75, 103, 0, 0), ("row", 103, 128, 0, 0), ("sum", 75, 128, 0, 0)],
-    "PEN": "a", "OWND": False,
-    "cyc": 1.04, "pe": 0.52, "gat": 1.5, "tt2": 1.0, "sem": 70.0, "issue": 600.0, "land": 2200.0, "fix": 60.0, "peu": 400,
-    "lag": 3000.0, "seed": 3, "tries": 800, "temp": 200.0,
-    "cases": [{}, {"cyc": 0.9, "pe": 0.45, "gat": 1.1, "sem": 50.0, "land": 1600.0},
-              {"cyc": 1.2, "pe": 0.6, "gat": 2.0, "sem": 100.0, "land": 3000.0, "tt2": 2.0}],
+    "KC": [24, 128],
+    "SG": [(24, 80, "a"), (80, 128, "v")],
+    "FG": [(0, 42, "v"), (42, 74, "a"), (74, 105, "a")],
+    "TL": [("max", 24, 65), ("row", 65, 97), ("row", 97, 128), ("sum", 65, 128)],
+    "cyc": 0.9, "pe": 0.45, "gat": 1.5, "tt2": 1.0, "sem": 160.0, "issue": 600.0, "land": 2600.0, "fix": 90.0, "vfix": 50.0, "peu": 400,
+    "lag": 3000.0, "seed": 3, "tries": 450, "temp": 200.0,
+    "cases": [{"cyc": 0.83, "pe": 0.42, "sem": 170.0, "fix": 70.0, "vfix": 40.0}, {"cyc": 0.83, "pe": 0.42, "sem": 110.0, "fix": 150.0, "vfix": 80.0},
+              {"cyc": 1.15, "pe": 0.58, "gat": 1.7, "sem": 170.0, "fix": 70.0, "vfix": 40.0, "land": 2800.0, "tt2": 2.0}],
 }
 NCH = len(CFG["KC"]) - 1
 REG, OWN, STR, ZED, EM = 416, 80, 288, 416, 136
 F32, BF, F16, I32, U16 = "float32", "bfloat16", "float16", "int32", "uint16"
-SCRATCH = {
-    "bk": ("sbuf", [128, W], BF), "ar": ("sbuf", [128, 256], I32), "ln": ("sbuf", [128, 4], I32), "ti": ("sbuf", [128, 4], I32),
-    "win": ("sbuf", [128, REG * 2 * RO + 8], F32), "em": ("sbuf", [128, EM * 2 * RO], BF), "el": ("sbuf", [128, EM * 2 * RO], BF),
-    "thf": ("sbuf", [128, 2], F32), "par": ("sbuf", [128, 256], I32), "sgn": ("sbuf", [128, 256], F32),
-    "iot": ("sbuf", [128, 144], BF), "nio": ("sbuf", [128, 104], BF), "low": ("sbuf", [128, 104], BF),
-    "pmi": ("sbuf", [128, 128], BF), "blk": ("sbuf", [128, 128], BF), "bm": ("sbuf", [128, 128], BF),
-    "pid": ("sbuf", [128, 2], I32), "pc": ("sbuf", [128, 8], F32),
-    "idp": ("sbuf", [128, 128], BF), "idn": ("sbuf", [128, 128], BF), "idm": ("sbuf", [128, 128], BF), "idb": ("sbuf", [128, 128], BF),
-    "dcl": ("sbuf", [128, 2048], BF), "wp": ("sbuf", [128, 144], BF), "w2": ("sbuf", [128, 144], BF), "wn": ("sbuf", [128, 144], BF),
-    "dg": ("sbuf", [128, 16], F32), "fp": ("sbuf", [128, 16], BF), "fn": ("sbuf", [128, 16], BF), "cm": ("sbuf", [128, 128], F32),
-    "yo": ("sbuf", [128, 256], F32), "yl": ("sbuf", [128, 2], F32), "yb": ("sbuf", [128, 2], F32),
-}
+SCRATCH = {}
+for _n, _c, _d in (("bk", W, BF), ("ar", 256, I32), ("ln", 4, I32), ("ti", 4, I32), ("win", REG * 2 * RO + 8, F32), ("em", EM * 2 * RO, BF),
+                   ("el", EM * 2 * RO, BF), ("thf", 2, F32), ("par", 256, I32), ("sgn", 256, F32), ("iot", 144, BF), ("nio", 104, BF),
+                   ("low", 104, BF), ("pmi", 128, BF), ("blk", 128, BF), ("bm", 128, BF), ("pid", 2, I32), ("pc", 8, F32), ("idp", 128, BF),
+                   ("idn", 128, BF), ("idm", 128, BF), ("idb", 128, BF), ("dcl", 2048, BF), ("wp", 144, BF), ("w2", 144, BF), ("wn", 144, BF),
+                   ("dg", 16, F32), ("fp", 16, BF), ("fn", 16, BF), ("cm", 128, F32), ("yo", 256, F32), ("yl", 2, F32), ("yb", 2, F32)):
+    SCRATCH[_n] = ("sbuf", [128, _c], _d)
 for _s in range(2):
     for _n, _c, _d in (("va", 128, F32), ("vb", 128, F32), ("y0", 128, F32), ("xs", 128, F32), ("mq", 128, F32), ("rr", 128, F32),
                        ("si", 128, I32), ("hi", 128, I32), ("ho", 106, U16), ("R", 1680, BF), ("AB", 1664, BF), ("G", 1664, F16),
                        ("xm", 128, F16), ("mz", 128, F16), ("aa", 104, F16), ("uu", 104, F16), ("off", 104, U16), ("pen", 104, BF),
-                       ("sm", 16, F32), ("ai", 8, F32), ("oq", 2, U16), ("orr", 2, U16), ("l8", 8, U16), ("gq", 16, F32), ("gr", 16, BF)):
+                       ("sm", 16, F32), ("ai", 8, F32), ("oq", 2, U16), ("orr", 2, U16), ("l8", 8, U16),
+                       ("gq", 16, F32), ("dv", 104, F32), ("gr", 16, BF)):
         SCRATCH["%s%d" % (_n, _s)] = ("sbuf", [128, _c], _d)
     SCRATCH["K%d" % _s] = ("psum", [128, 512], F32)
     for _c in range(NCH):
@@ -41,8 +35,7 @@ for _s in range(2):
 ND = 6 - 2 * NCH
 for _c in range(ND):
     SCRATCH["D%d" % _c] = ("psum", [128, 512], F32)
-NDMA = 10
-SEMAPHORES = (["cv", "ca", "cp", "cg", "sent"] + ["d%d" % i for i in range(NDMA)]
+SEMAPHORES = (["cv", "ca", "cp", "cg", "sent"] + ["d%d" % i for i in range(10)]
               + ["a%s%d%d" % (k, t, s) for k in "SE" for t in range(RO) for s in range(2)])
 A, ACT = AluOpType, ActivationFunctionType
 M12, M7 = 1.5 * 2.0 ** 35, 1.5 * 2.0 ** 30
@@ -69,7 +62,7 @@ def build():
         return all(SCRATCH[v[0]][2] in (BF, F16, U16) for v in vs)
 
     def vcost(n, f):
-        return max(64, n * f) * cyc
+        return max(64, n * f) * cyc + CFG["vfix"]
 
     def ts(out, in0, s1, s2, op0, op1=None):
         add("v", "ts", (out, in0, s1, s2, op0, op1), [in0, s1, s2], [out], vcost(cols(out), 0.5 if two(out, in0) else 1))
@@ -86,6 +79,9 @@ def build():
 
     def fill(out, c):
         add("v", "fill", (out, c), [], [out], vcost(cols(out), 0.5 if two(out) else 1))
+
+    def scan(out, d0, d1, ini, op):
+        add("v", "scan", (out, d0, d1, ini, op), [d0, d1, ini], [out], vcost(cols(out), 1))
 
     def act(out, in0, func, bias=0.0, scale=1.0):
         add("a", "act", (out, in0, func, bias, scale), [in0, bias, scale], [out], CFG["fix"] + cols(out) * cyc)
@@ -136,8 +132,7 @@ def build():
     ts(V("low"), V("iot", LO, M), -1.0, 75.5, A.mult, A.add)
     for name, c in (("idp", 1.0), ("idn", -1.0), ("idm", 2.0 ** -9), ("idb", -2.0 ** 20)):
         ts(V(name), V("pmi"), 0.0, c, A.is_equal, A.mult)
-    modes = [x[0] for x in CFG["TL"]]
-    for name, c in (("wp", 128.0),) + ((("w2", 256.0), ("wn", -128.0)) if "max" in modes else ()):
+    for name, c in (("wp", 128.0), ("w2", 256.0), ("wn", -128.0)):
         ts(V(name), V("iot"), P15, c, A.is_equal, A.mult)
     ts(V("pmi"), V("pmi"), 0.0, -1.0 / 64, A.is_equal, A.mult)
     for cl in range(16):
@@ -153,9 +148,14 @@ def build():
     def ends(t, s):
         B = lambda n, lo=0, hi=None, st=1: V("%s%d" % (n, s), lo, hi, st)
         e0 = EM * (2 * t + s)
-        gat("v", B("gq"), B("va"), B("oq", 0, 1), V("dg"))
-        red(B("sm", 2, 3), B("gq"), A.add)
-        ts(B("l8"), V("cm", 0, 8), B("sm", 2, 3), None, A.add)
+        if t == 0:
+            gat("v", B("gq"), B("va"), B("oq", 0, 1), V("dg"))
+            red(B("sm", 2, 3), B("gq"), A.add)
+            ts(B("l8"), V("cm", 0, 8), B("sm", 2, 3), None, A.add)
+        else:
+            ts(B("mq", 0, 104), V("K%d" % s, 0, 104), B("sm", 0, 1), 8192.0, A.subtract, A.mult)
+            scan(B("rr", 0, 104), B("mq", 0, 104), B("dv"), -1e9, A.max)
+            ts(B("l8"), V("cm", 0, 8), B("rr", 103, 104), B("va", M - 1, M), A.add, A.add)
         gat("v", V("em", e0, e0 + 128), V("bk"), B("l8"), V("bm"))
         send("E", t, s, V("em", e0, e0 + 130), V("el", e0, e0 + 130))
 
@@ -202,17 +202,14 @@ def build():
                 for a, b, eng in CFG["SG"]:
                     if lo <= a < hi:
                         gat(eng, B("G", 16 * (a - LO), 16 * (b - LO)), V("win", w0, w0 + REG + 8), B("off", a - LO, b - LO))
-                cuts = [k for k in CFG["SX"] if max(lo, LO) <= k <= hi]
+                a = max(lo, LO)
                 mm([(V(X, lo, hi), V("idm"), B("xm", lo, hi), True, False)])
-                for a, b in zip(cuts, cuts[1:]):
-                    mm([(V(X, a, b), V("dcl", 128 * cl, 128 * cl + 128), B("G", 16 * (a - LO) + cl, 16 * (b - LO), 16), False,
-                         cl == 15 and b == cuts[-1]) for cl in range(16)])
+                mm([(V(X, a, hi), V("dcl", 128 * cl, 128 * cl + 128), B("G", 16 * (a - LO) + cl, 16 * (hi - LO), 16), False, cl == 15)
+                    for cl in range(16)])
             for c, (lo, hi, X) in enumerate(rng):
                 hl = max(lo, LO - 1)
                 act(B("va", lo, hi), V(X, lo, hi), ACT.Abs, 0.5, 128.0)
-                ini = B("ai", t, t + 1) if c == 0 else B("sm", 8 + c, 9 + c)
-                add("v", "scan", (V(X, 128 + lo, 128 + hi), V("cm", lo, hi), B("va", lo, hi), ini),
-                    [V("cm", lo, hi), B("va", lo, hi), ini], [V(X, 128 + lo, 128 + hi)], vcost(hi - lo, 1))
+                scan(V(X, 128 + lo, 128 + hi), V("cm", lo, hi), B("va", lo, hi), B("ai", t, t + 1) if c == 0 else B("sm", 8 + c, 9 + c), A.add)
                 ts(B("mq", hl, hi), V(X, 128 + hl, 128 + hi), M12, M12, A.add, A.subtract)
                 tt(B("rr", hl, hi), V(X, 128 + hl, 128 + hi), B("mq", hl, hi), A.subtract)
                 if c + 1 < NCH:
@@ -225,35 +222,26 @@ def build():
                 if t + 1 < RO:
                     act(V("win", w1 + OWN + lo, w1 + OWN + hi), V(X, lo, hi), ACT.Copy, 0.0, 64.0)
             if t + 1 < RO:
+                tt(B("dv"), B("va", LO - 1, M - 1), B("va", LO, M), A.subtract)
                 send("S", t + 1, s, V("win", w1 + OWN, w1 + OWN + M), V("win", w1 + STR, w1 + STR + M))
             else:
                 act(B("y0"), B("va"), ACT.Identity, -1.5)
-            if CFG["PEN"] == "a":
-                act(B("pen"), B("va", LO, M), ACT.Relu, 1.5, -1.0)
-            else:
-                ts(B("pen"), B("va", LO, M), 0.5, None, A.is_equal)
+            act(B("pen"), B("va", LO, M), ACT.Relu, 1.5, -1.0)
             mm([(V(K, 0, 104), V("idp"), V("low"), True, False), (V(K, 0, 104), V("idb"), B("pen"), False, False)])
             for a, b, eng in CFG["FG"]:
                 gat(eng, B("R", 16 * a, 16 * b), V("bk"), B("ho", a, b))
             TL, at = CFG["TL"], 0
-            for ti, (mode, a, b, c0, c1) in enumerate(TL):
+            for ti, (mode, a, b) in enumerate(TL):
                 j0, j1, o, wd, fin = 16 * (a - LO), 16 * (b - LO), V(K, a - LO, b - LO), b - a, ti + 1 == len(TL)
                 sel = lambda n, cl: V(n, 15 - cl, 143 - cl)
-                if mode in ("abs", "row"):
-                    D = "D%d" % (s * (ND // 2) + tile[0] % (ND // 2) if CFG["OWND"] else tile[0] % ND)
-                    tile[0] += 1
                 if mode == "max":
                     tt(B("AB", at, at + 16 * wd), B("R", j0 + 16, j1 + 16), B("R", j0, j1), A.max)
                     mm([(o, sel("wn", cl), B("R", j0 + u + cl, j1 + u, 16), False, False) for cl in range(16) for u in (0, 16)])
                     mm([(o, sel("w2", cl), B("AB", at + cl, at + 16 * wd, 16), False, fin and cl == 15) for cl in range(16)])
                     at += 16 * wd
-                elif mode == "abs":
-                    mm([(V(D, (cl - c0) * wd, (cl - c0 + 1) * wd), V(nm), B("R", j0 + u + cl, j1 + u, 16), u == 16, u == 0)
-                        for cl in range(c0, c1) for nm, u in (("idp", 16), ("idn", 0))])
-                    act(B("AB", at, at + (c1 - c0) * wd), V(D, 0, (c1 - c0) * wd), ACT.Abs)
-                    mm([(o, sel("wp", cl), B("AB", at + (cl - c0) * wd, at + (cl - c0 + 1) * wd), False, fin and cl == c1 - 1) for cl in range(c0, c1)])
-                    at += (c1 - c0) * wd
                 elif mode == "row":
+                    D = "D%d" % (tile[0] % ND)
+                    tile[0] += 1
                     mm([(V(D, 0, j1 - j0), V("idp"), B("R", j0 + 16, j1 + 16), True, False), (V(D, 0, j1 - j0), V("idn"), B("R", j0, j1), False, True)])
                     act(B("AB", at, at + 16 * wd), V(D, 0, j1 - j0), ACT.Abs)
                     at += 16 * wd
@@ -264,7 +252,6 @@ def build():
             ts(q_, m_, M7, M7, A.add, A.subtract)
             if t + 1 < RO:
                 nn = V("em", e0 + 2 * EM + 128, e0 + 2 * EM + 129)
-                ts(B("oq", 0, 1), q_, m_, 74.5, A.subtract, A.add)
                 ts(nn, q_, m_, 75.5, A.subtract, A.add)
                 ends(t + 1, s)
             else:
@@ -378,7 +365,7 @@ def plan():
         for i, o in enumerate(ops):
             if o["kind"] == "load":
                 bias[i] = 1e6 * (20 - i)
-        per = [i for i, o in enumerate(ops) if o["kind"] == "scan"]
+        per = [i for i, o in enumerate(ops) if o["kind"] == "scan" and o["args"][4] == A.add]
         per = per[NCH] - per[0]
         now, best = 1e30, None
         for it in range(CFG["tries"] + 1):
@@ -461,7 +448,7 @@ def rank_program(g, core, T, topo):
         elif kind == "fill":
             ins = q.memset(ap(x[0]), x[1])
         elif kind == "scan":
-            ins = q.tensor_tensor_scan(ap(x[0]), ap(x[1]), ap(x[2]), ap(x[3]), A.add, A.add)
+            ins = q.tensor_tensor_scan(ap(x[0]), ap(x[1]), ap(x[2]), ap(x[3]), x[4], A.add)
         elif kind == "act":
             ins = q.activation(ap(x[0]), ap(x[1]), x[2], bias=ap(x[3]), scale=ap(x[4]))
         elif kind == "gat":

@@ -4,30 +4,35 @@ from concourse.mybir import AluOpType, AxisListType, ActivationFunctionType
 RO, M, LO, W, NR = 5, 128, 24, 4096, 8
 CFG = {
     "KC": [24, 128],
-    "SG": [(24, 80, "a"), (80, 128, "v")],
-    "FG": [(0, 42, "v"), (42, 74, "a"), (74, 105, "a")],
-    "TL": [("max", 24, 65), ("row", 65, 97), ("row", 97, 128), ("sum", 65, 128)],
+    "DG": [24, 76, 128],
+    "SG": [(24, 50, "a"), (50, 76, "v"), (76, 102, "a"), (102, 128, "v")],
+    "FG": [(0, 20, "v"), (20, 72, "a"), (72, 90, "v"), (90, 105, "v")],
+    "TL": [("row", 24, 43), ("row", 43, 69), ("sum", 24, 69), ("row", 69, 95), ("row", 95, 113), ("row", 113, 128), ("sum", 69, 128)],
+    "eng": {"mq": "v", "pen": "v", "E": "v", "gr": "a", "dcl": "a"},
     "cyc": 0.9, "pe": 0.45, "gat": 1.5, "tt2": 1.0, "sem": 160.0, "issue": 600.0, "land": 2600.0, "fix": 90.0, "vfix": 50.0, "peu": 400,
-    "lag": 3000.0, "seed": 3, "tries": 450, "temp": 200.0,
+    "first": 1200.0, "lag": 2000.0, "seed": 3, "steps": 30000, "temp": 30.0,
     "cases": [{"cyc": 0.83, "pe": 0.42, "sem": 170.0, "fix": 70.0, "vfix": 40.0}, {"cyc": 0.83, "pe": 0.42, "sem": 110.0, "fix": 150.0, "vfix": 80.0},
               {"cyc": 1.15, "pe": 0.58, "gat": 1.7, "sem": 170.0, "fix": 70.0, "vfix": 40.0, "land": 2800.0, "tt2": 2.0}],
 }
 NCH = len(CFG["KC"]) - 1
-REG, OWN, STR, ZED, EM = 416, 80, 288, 416, 136
+REG, OWN, STR = 424, 88, 296
+EM, EE, EL = 240, 112, 136
 F32, BF, F16, I32, U16 = "float32", "bfloat16", "float16", "int32", "uint16"
 SCRATCH = {}
-for _n, _c, _d in (("bk", W, BF), ("ar", 256, I32), ("ln", 4, I32), ("ti", 4, I32), ("win", REG * 2 * RO + 8, F32), ("em", EM * 2 * RO, BF),
-                   ("el", EM * 2 * RO, BF), ("thf", 2, F32), ("par", 256, I32), ("sgn", 256, F32), ("iot", 144, BF), ("nio", 104, BF),
-                   ("low", 104, BF), ("pmi", 128, BF), ("blk", 128, BF), ("bm", 128, BF), ("pid", 2, I32), ("pc", 8, F32), ("idp", 128, BF),
-                   ("idn", 128, BF), ("idm", 128, BF), ("idb", 128, BF), ("dcl", 2048, BF), ("wp", 144, BF), ("w2", 144, BF), ("wn", 144, BF),
-                   ("dg", 16, F32), ("fp", 16, BF), ("fn", 16, BF), ("cm", 128, F32), ("yo", 256, F32), ("yl", 2, F32), ("yb", 2, F32)):
+for _n, _c, _d in (("bk", W + 16, BF), ("ar", 256, I32), ("ln", 4, I32), ("ti", 4, I32), ("win", REG * 2 * RO, F32), ("em", EM * 2 * RO, BF),
+                   ("el", EL * 2 * RO, BF), ("thf", 2, F32), ("ea", 256, I32), ("iot", 144, BF), ("low", 104, BF), ("pmi", 128, BF),
+                   ("blk", 128, BF), ("bm", 128, BF), ("pid", 2, I32), ("pc", 8, F32), ("idp", 128, BF), ("idn", 128, BF), ("id2", 128, BF),
+                   ("idb", 128, BF), ("idf", 128, F32), ("one", 104, F32), ("dcl", 2048, BF), ("wp", 144, BF), ("w2", 144, BF),
+                   ("wn", 144, BF), ("w1", 144, BF), ("dg", 16, F32), ("fp", 16, BF), ("fn", 16, BF), ("od", 18, BF), ("cd", 18, BF),
+                   ("cc", 128, BF), ("cq", 128, F32), ("cm", 104, F32), ("dl", 104, F32), ("cz", 104, F32), ("bo", 8, F32),
+                   ("yo", 256, F32), ("yl", 208, F32), ("yb", 2, F32)):
     SCRATCH[_n] = ("sbuf", [128, _c], _d)
 for _s in range(2):
-    for _n, _c, _d in (("va", 128, F32), ("vb", 128, F32), ("y0", 128, F32), ("xs", 128, F32), ("mq", 128, F32), ("rr", 128, F32),
-                       ("si", 128, I32), ("hi", 128, I32), ("ho", 106, U16), ("R", 1680, BF), ("AB", 1664, BF), ("G", 1664, F16),
-                       ("xm", 128, F16), ("mz", 128, F16), ("aa", 104, F16), ("uu", 104, F16), ("off", 104, U16), ("pen", 104, BF),
-                       ("sm", 16, F32), ("ai", 8, F32), ("oq", 2, U16), ("orr", 2, U16), ("l8", 8, U16),
-                       ("gq", 16, F32), ("dv", 104, F32), ("gr", 16, BF)):
+    for _n, _c, _d in (("pp", 128, F32), ("sq", 128, F32), ("y0", 128, F32), ("xs", 128, F16), ("ev", 128, F16), ("mq", 128, BF),
+                       ("mc", 104, F32), ("rr", 104, F32), ("si", 128, I32), ("hi", 128, I32), ("ho", 106, U16), ("R", 1680, BF),
+                       ("AB", 1664, BF), ("G", 1664, F16), ("xm", 128, F16), ("mz", 104, F16), ("off", 104, U16), ("pen", 104, BF),
+                       ("nc", 104, BF), ("sm", 16, F32), ("ai", 8, F32), ("oq", 2, U16), ("orr", 2, U16), ("l8", 8, U16),
+                       ("gq", 18, F32), ("gr", 16, BF)):
         SCRATCH["%s%d" % (_n, _s)] = ("sbuf", [128, _c], _d)
     SCRATCH["K%d" % _s] = ("psum", [128, 512], F32)
     for _c in range(NCH):
@@ -38,7 +43,8 @@ for _c in range(ND):
 SEMAPHORES = (["cv", "ca", "cp", "cg", "sent"] + ["d%d" % i for i in range(10)]
               + ["a%s%d%d" % (k, t, s) for k in "SE" for t in range(RO) for s in range(2)])
 A, ACT = AluOpType, ActivationFunctionType
-M12, M7 = 1.5 * 2.0 ** 35, 1.5 * 2.0 ** 30
+M12, M1 = 1.5 * 2.0 ** 35, 1.5 * 2.0 ** 24
+MARK, GAP = 4096.0, 8192.0
 
 
 def V(name, lo=0, hi=None, step=1):
@@ -50,12 +56,16 @@ def cols(v):
 
 
 def build():
-    ops, cur = [], [0]
-    cyc = CFG["cyc"]
+    ops, cur, sent = [], [0], []
+    cyc, ENG = CFG["cyc"], CFG["eng"]
 
     def add(eng, kind, args, reads, writes, cost, lat=0.0, after=()):
         ops.append({"eng": eng, "kind": kind, "args": args, "r": [x for x in reads if isinstance(x, tuple)], "w": list(writes),
                     "cost": cost, "lat": lat, "after": list(after), "s": cur[0], "succ": []})
+        if len(cur) > 1:
+            key = (cur[0], eng, kind, (ops[-1]["w"] or ops[-1]["r"])[0][0])
+            cur[1][key] = cur[1].get(key, 0) + 1
+            ops[-1]["tag"] = key + (cur[1][key],)
         return len(ops) - 1
 
     def two(*vs):
@@ -74,8 +84,8 @@ def build():
     def cp(out, in0):
         add("v", "cp", (out, in0), [in0], [out], vcost(cols(out), 0.5 if two(out, in0) else 1))
 
-    def red(out, in0, op, ab=False):
-        add("v", "red", (out, in0, op, ab), [in0], [out], vcost(cols(in0), 1))
+    def red(out, in0, op, ab=False, neg=False):
+        add("v", "red", (out, in0, op, ab, neg), [in0], [out], vcost(cols(in0), 1))
 
     def fill(out, c):
         add("v", "fill", (out, c), [], [out], vcost(cols(out), 0.5 if two(out) else 1))
@@ -83,8 +93,9 @@ def build():
     def scan(out, d0, d1, ini, op):
         add("v", "scan", (out, d0, d1, ini, op), [d0, d1, ini], [out], vcost(cols(out), 1))
 
-    def act(out, in0, func, bias=0.0, scale=1.0):
-        add("a", "act", (out, in0, func, bias, scale), [in0, bias, scale], [out], CFG["fix"] + cols(out) * cyc)
+    def act(out, in0, func, bias=0.0, scale=1.0, acc=None):
+        add("a", "act", (out, in0, func, bias, scale, acc), [in0, bias, scale], [out] + ([acc] if acc else []),
+            CFG["fix"] + cols(out) * cyc + (20 if acc else 0))
 
     def gat(eng, out, win, off, mask=None):
         add(eng, "gat", (out, win, off, mask), [win, off, mask], [out], 60 + cols(out) * CFG["gat"] * cyc)
@@ -93,7 +104,7 @@ def build():
         while lst:
             k, c = 0, 0
             while k < len(lst) and (c < CFG["peu"] or k % 2):
-                k, c = k + 1, c + max(64, cols(lst[k][2]))
+                k, c = k + 1, c + max(64, cols(lst[k][2])) * (4 if SCRATCH[lst[k][2][0]][2] == F32 else 1)
             add("p", "mm", lst[:k], [x[1] for x in lst[:k]] + [x[2] for x in lst[:k]], [x[0] for x in lst[:k]], c * CFG["pe"], 60.0)
             lst = lst[k:]
 
@@ -104,7 +115,8 @@ def build():
         add(eng, "load", (out, name, lo, hi), [], [out], 60.0, lat)
 
     def send(kind, t, s, src, dst):
-        i = add("g", "send", (kind, t, s, src, dst), [src], [], CFG["issue"])
+        sent.append(add("g", "send", (kind, t, s, src, dst), [src], [], CFG["issue"] + (0 if sent else CFG["first"]), after=sent[:1]))
+        i = sent[-1]
         add(None, "arr", "a%s%d%d" % (kind, t, s), [], [dst], 0.0, CFG["land"] + (500 if kind == "S" else 0), after=[i])
 
     load("s", V("ar"), "arms", 0, 256, 2200.0)
@@ -121,151 +133,178 @@ def build():
     cp(CL, V("pid", 1, 2))
     ts(P16, V("pid", 0, 1), CL, None, A.subtract)
     ts(P15, P16, 15.0, None, A.add)
-    ts(CLR, CL, -16.0 * (LO - 1), None, A.add)
+    ts(CLR, CL, 16.0 * (M - LO + 1), None, A.add)
     ts(V("dg"), V("iot", 0, 16), CL, None, A.is_equal)
     ts(V("bm"), V("blk"), P16, None, A.is_equal)
-    fill(V("cm"), -1.5)
-    fill(V("em", 129, EM * 2 * RO, EM), 0.0)
+    ts(V("bo"), V("bm", 0, 128, 16), -GAP, GAP + W // 2, A.mult, A.add)
+    fill(V("bk", W, W + 16), 0.0)
+    fill(V("cq"), 0.25)
+    fill(V("cm"), -1.0)
+    fill(V("em", EE - 2, 2 * EM, EM), 0.0)
     ts(V("fp"), V("iot", 0, 16), CL, None, A.is_equal)
     ts(V("fn"), V("iot", 0, 16), CL, -1.0, A.is_equal, A.mult)
-    ts(V("nio"), V("iot", LO, M), -1.0, OWN - 1.0, A.mult, A.add)
-    ts(V("low"), V("iot", LO, M), -1.0, 75.5, A.mult, A.add)
-    for name, c in (("idp", 1.0), ("idn", -1.0), ("idm", 2.0 ** -9), ("idb", -2.0 ** 20)):
+    ts(V("pc", 4, 5), V("dg", 0, 1), W // 2, None, A.mult)
+    ts(V("pc", 5, 6), V("dg", 1, 2), -0.25, V("pc", 4, 5), A.mult, A.add)
+    ts(V("cc"), V("iot", 0, 128), 0.0, V("pc", 5, 6), A.mult, A.add)
+    fill(V("cd", 0, 16), 0.0)
+    fill(V("cd", 16, 17), float(M + OWN))
+    fill(V("cd", 17, 18), float(STR - OWN))
+    ts(V("od"), V("iot", 0, 18), CL, -GAP, A.not_equal, A.mult)
+    fill(V("od", 16, 18), 0.0)
+    ts(V("low"), V("iot", LO, M), -GAP, None, A.mult)
+    for name, c in (("idp", 1.0), ("idn", -1.0), ("id2", 2.0), ("idb", -2.0 ** (33 if ENG["pen"] == "v" else 22)), ("idf", 1.0)):
         ts(V(name), V("pmi"), 0.0, c, A.is_equal, A.mult)
-    for name, c in (("wp", 128.0), ("w2", 256.0), ("wn", -128.0)):
-        ts(V(name), V("iot"), P15, c, A.is_equal, A.mult)
-    ts(V("pmi"), V("pmi"), 0.0, -1.0 / 64, A.is_equal, A.mult)
+    for name, c in (("wp", 128 * GAP), ("w2", 256 * GAP), ("wn", -128 * GAP), ("w1", 1.0)):
+        if name in ("wp", "w1") or any(x[0] == "max" for x in CFG["TL"]):
+            ts(V(name), V("iot"), P15, c, A.is_equal, A.mult)
     for cl in range(16):
-        act(V("dcl", 128 * cl, 128 * cl + 128), V("pmi"), ACT.Copy, 0.0, V("dg", cl, cl + 1))
-    cp(V("thf"), V("ti", 0, 2))
-    ts(V("par"), V("ar"), 1, None, A.bitwise_and)
-    ts(V("sgn"), V("par"), -0.5, None, A.add)
-    fill(V("win", 0, OWN), 0.0)
-    for i in range(2 * RO):
-        fill(V("win", REG * i + OWN + M, REG * i + STR), 0.0)
-        fill(V("win", REG * (i + 1), min(REG * (i + 1) + OWN, REG * 2 * RO + 8)), 0.0)
-
-    def ends(t, s):
-        B = lambda n, lo=0, hi=None, st=1: V("%s%d" % (n, s), lo, hi, st)
-        e0 = EM * (2 * t + s)
-        if t == 0:
-            gat("v", B("gq"), B("va"), B("oq", 0, 1), V("dg"))
-            red(B("sm", 2, 3), B("gq"), A.add)
-            ts(B("l8"), V("cm", 0, 8), B("sm", 2, 3), None, A.add)
+        if ENG["dcl"] == "a":
+            act(V("dcl", 128 * cl, 128 * cl + 128), V("idp"), ACT.Copy, 0.0, V("dg", cl, cl + 1))
         else:
-            ts(B("mq", 0, 104), V("K%d" % s, 0, 104), B("sm", 0, 1), 8192.0, A.subtract, A.mult)
-            scan(B("rr", 0, 104), B("mq", 0, 104), B("dv"), -1e9, A.max)
-            ts(B("l8"), V("cm", 0, 8), B("rr", 103, 104), B("va", M - 1, M), A.add, A.add)
-        gat("v", V("em", e0, e0 + 128), V("bk"), B("l8"), V("bm"))
-        send("E", t, s, V("em", e0, e0 + 130), V("el", e0, e0 + 130))
+            ts(V("dcl", 128 * cl, 128 * cl + 128), V("idp"), V("dg", cl, cl + 1), None, A.mult)
+    cp(V("thf"), V("ti", 0, 2))
+    ts(V("ea"), V("ar"), W - 2, None, A.bitwise_and)
+    cp(V("yo", 0, 2 * LO), V("ar", 0, 2 * LO))
+    fill(V("win", 0, REG * 2 * RO, REG), 0.0)
+    for i in range(2 * RO):
+        for a in (OWN, STR):
+            if i < 2:
+                fill(V("win", REG * i + a - 80, REG * i + a), MARK)
+            else:
+                iota(V("win", REG * i + a - 80, REG * i + a), [[0, 80]], int(MARK), 0)
+    iota(V("one"), [[0, 104]], 1, 0)
+    iota(V("cz"), [[0, 104]], 0, 0)
+    iota(V("dl", 0, 103), [[0, 103]], -1, 0)
+    iota(V("dl", 103, 104), [[0, 1]], M - 1, 0)
 
-    def gain(t, s):
-        K = "K%d" % s
-        mm([(V(K, 108, 109), V("wp", 15 - cl, 143 - cl), V("gr%d" % s, cl, cl + 1), cl == 0, cl == 15) for cl in range(16)])
-        act(V("ai%d" % s, t + 1, t + 2), V(K, 108, 109), ACT.Identity, V("ai%d" % s, t, t + 1), 1.0 / 128)
+    def ends(t, s, code):
+        e0, l0 = EM * (2 * t + s) + EE, EL * (2 * t + s) + 8
+        ts(V("l8%d" % s), V("bo"), code, float(W), A.add, A.min)
+        gat(ENG["E"], V("em", e0, e0 + 128), V("bk"), V("l8%d" % s))
+        send("E", t, s, V("em", e0 - 2, e0 + 128), V("el", l0 - 2, l0 + 128))
 
     for s in range(2):
         B = lambda n, lo=0, hi=None, st=1: V("%s%d" % (n, s), lo, hi, st)
         w0, cur[0] = REG * s, s
-        ts(B("va"), V("ar", s, 256, 2), 1.5, None, A.add)
-        tt(B("y0"), B("va"), V("sgn", s, 256, 2), A.mult)
-        ts(V("win", w0 + OWN, w0 + OWN + M), B("y0"), -0.25, None, A.add)
+        n_ = V("em", EM * s + EE - 1, EM * s + EE)
+        ts(B("xs"), V("ar", s, 256, 2), -float(W // 2), None, A.add)
+        ts(B("pp"), V("ea", s, 256, 2), 2.0, 1.0 - W, A.mult, A.add)
+        tt(V("win", w0 + OWN, w0 + OWN + M), B("pp"), B("xs"), A.subtract)
         send("S", 0, s, V("win", w0 + OWN, w0 + OWN + M), V("win", w0 + STR, w0 + STR + M))
-        act(B("xs"), V("win", w0 + OWN, w0 + OWN + M), ACT.Copy, 0.0, 1.0 / 64)
-        cp(V("em", EM * s + 128, EM * s + 129), V("ln", s, s + 1))
+        act(B("y0"), B("xs"), ACT.Copy)
+        ts(n_, V("ln", s, s + 1), -float(M), None, A.add)
         ts(B("oq", 0, 1), V("ln", s, s + 1), -1.0, None, A.add)
-        fill(B("ai", 0, 1), -2047.5)
-        ends(0, s)
+        gat("v", B("gq", 0, 16), B("y0"), B("oq", 0, 1), V("dg"))
+        red(B("sm", 2, 3), B("gq", 0, 16), A.add)
+        ends(0, s, B("sm", 2, 3))
+        cp(B("ev", 0, LO), V("ea", s, 2 * LO, 2))
+        cp(B("xm", LO - 1, LO), B("xs", LO - 1, LO))
+        red(B("sm", 6, 7), B("y0", 0, LO - 1), A.add)
+        ts(B("ai", 0, 1), B("sm", 6, 7), (LO - 1) * (W // 2) + 2048.5, None, A.add)
+        ts(B("rr"), V("low"), 1.0 / GAP, n_, A.mult, A.add)
+        ts(B("mc"), B("rr"), -float(M), -GAP, A.is_gt, A.mult)
+        ts(B("rr"), B("rr"), float(M - 1), None, A.add)
+        tt(B("nc"), B("rr"), B("mc"), A.add)
 
     KC = CFG["KC"]
     tile = [0]
     for t in range(RO):
         for s in range(2):
             B = lambda n, lo=0, hi=None, st=1: V("%s%d" % (n, s), lo, hi, st)
-            e0, w0, w1 = EM * (2 * t + s), REG * (2 * t + s), REG * (2 * t + 2 + s)
-            n_, n2 = V("em", e0 + 128, e0 + 129), V("el", e0 + 128, e0 + 129)
-            K, cur[0] = "K%d" % s, s
-            rng = [(0 if c == 0 else KC[c], KC[c + 1], "X%d%d" % (s, c)) for c in range(NCH)]
-            ts(B("mz"), V("iot", 0, M), n_, 512.0, A.is_lt, A.mult)
-            ts(B("aa"), V("nio"), n_, n_, A.add, A.add)
-            tt(B("uu"), B("aa"), B("mz", LO, M), A.add)
-            for lo, hi, X in rng:
-                tt(B("xm", lo, hi), B("xs", lo, hi) if t == 0 else V(X, lo, hi), B("mz", lo, hi), A.mult)
-            mm([(V(K, 112, 128), V("em", e0, e0 + 128), V("fp"), True, False), (V(K, 112, 128), V("el", e0, e0 + 128), V("fn"), False, True)])
-            ts(B("sm", 4, 5), n2, n_, float(STR - OWN), A.subtract, A.add)
-            red(B("sm", 3, 4), V(K, 112, 128), A.add, True)
-            ts(B("sm", 5, 6), B("sm", 3, 4), V("thf", s, s + 1), B("sm", 4, 5), A.is_lt, A.mult)
-            ts(B("off"), B("uu"), B("sm", 5, 6), float(ZED), A.add, A.min)
+            e0, l0, w0, w1 = EM * (2 * t + s) + EE, EL * (2 * t + s) + 8, REG * (2 * t + s), REG * (2 * t + 2 + s)
+            n_, n2 = V("em", e0 - 1, e0), V("el", l0 - 1, l0)
+            nc = V("em", e0 - 104, e0) if t else B("nc")
+            K, last = "K%d" % s, t + 1 == RO
+            cur[:] = [s, {}]
+            rng = [(LO - 1 if c == 0 else KC[c], KC[c + 1], "X%d%d" % (s, c)) for c in range(NCH)]
+            XL = rng[-1][2]
+            sel = lambda n, cl: V(n, 15 - cl, 143 - cl)
+            ts(B("mz"), nc, -1000.0, None, A.is_lt)
+            tt(B("xm", LO, M), B("xs", LO, M), B("mz"), A.mult)
             if t:
-                gain(t - 1, s)
+                ts(B("orr", 0, 1), n_, 16.0, CLR, A.mult, A.add)
+                gat(ENG["gr"], B("gr"), B("R"), B("orr", 0, 1))
+                mm([(V(K, 104, 121), V("idp"), V("od", 0, 17), True, False), (V(K, 120, 121), V("idf"), B("ai", t - 1, t), False, False),
+                    (V(K, 104, 120), V("bm"), B("gr"), False, True)])
+                act(B("gq", 0, 17), V(K, 104, 121), ACT.Relu, acc=B("ai", t, t + 1))
+            mm([(V(K, 128, 146), V("idp"), V("cd"), True, False), (V(K, 144, 145), V("idp"), n_, False, False),
+                (V(K, 145, 146), V("idn"), n_, False, False), (V(K, 128, 144), V("em", e0, e0 + 128), V("fp"), False, False)])
+            mm([(V(K, 145, 146), V("idp"), n2, False, False), (V(K, 128, 144), V("el", l0, l0 + 128), V("fn"), False, True)])
+            red(B("sm", 3, 4), V(K, 128, 144), A.add, True)
+            ts(B("sm", 5, 6), B("sm", 3, 4), V("thf", s, s + 1), V(K, 145, 146), A.is_lt, A.mult)
+            ts(B("off"), nc, B("sm", 5, 6), V(K, 144, 145), A.add, A.add)
+            for a, b, eng in CFG["SG"]:
+                gat(eng, B("G", 16 * (a - LO), 16 * (b - LO)), V("win", w0, w0 + REG), B("off", a - LO, b - LO))
             for lo, hi, X in rng:
-                for a, b, eng in CFG["SG"]:
+                mm([(V(X, lo, hi), V("bm"), V("cc", lo, hi), True, False), (V(X, lo, hi), V("idp"), B("xm", lo, hi), False, False)])
+                for a, b in zip(CFG["DG"], CFG["DG"][1:]):
                     if lo <= a < hi:
-                        gat(eng, B("G", 16 * (a - LO), 16 * (b - LO)), V("win", w0, w0 + REG + 8), B("off", a - LO, b - LO))
-                a = max(lo, LO)
-                mm([(V(X, lo, hi), V("idm"), B("xm", lo, hi), True, False)])
-                mm([(V(X, a, hi), V("dcl", 128 * cl, 128 * cl + 128), B("G", 16 * (a - LO) + cl, 16 * (hi - LO), 16), False, cl == 15)
-                    for cl in range(16)])
+                        mm([(V(X, a, b), V("dcl", 128 * cl, 128 * cl + 128), B("G", 16 * (a - LO) + cl, 16 * (b - LO), 16), False,
+                             cl == 15 and b == hi) for cl in range(16)])
             for c, (lo, hi, X) in enumerate(rng):
-                hl = max(lo, LO - 1)
-                act(B("va", lo, hi), V(X, lo, hi), ACT.Abs, 0.5, 128.0)
-                scan(V(X, 128 + lo, 128 + hi), V("cm", lo, hi), B("va", lo, hi), B("ai", t, t + 1) if c == 0 else B("sm", 8 + c, 9 + c), A.add)
-                ts(B("mq", hl, hi), V(X, 128 + hl, 128 + hi), M12, M12, A.add, A.subtract)
-                tt(B("rr", hl, hi), V(X, 128 + hl, 128 + hi), B("mq", hl, hi), A.subtract)
-                if c + 1 < NCH:
-                    cp(B("sm", 9 + c, 10 + c), V(X, 127 + hi, 128 + hi))
-                act(B("vb", hl, hi), B("va", hl, hi), ACT.Identity, -1.75)
-                act(V(X, 256 + hl, 256 + hi), B("rr", hl, hi), ACT.Square, 511.875, 0.25)
-                tt(B("si", hl, hi), V(X, 256 + hl, 256 + hi), B("vb", hl, hi), A.add)
-                ts(B("hi", hl, hi), B("si", hl, hi), W - 1, None, A.bitwise_and)
-                cp(B("ho", hl - LO + 1, hi - LO + 1), B("hi", hl, hi))
-                if t + 1 < RO:
-                    act(V("win", w1 + OWN + lo, w1 + OWN + hi), V(X, lo, hi), ACT.Copy, 0.0, 64.0)
-            if t + 1 < RO:
-                tt(B("dv"), B("va", LO - 1, M - 1), B("va", LO, M), A.subtract)
+                Z = V(K, 160 + lo, 160 + hi)
+                scan(B("pp", lo, hi), V("cq", lo, hi), V(X, lo, hi), B("ai", t, t + 1) if c == 0 else B("pp", lo - 1, lo), A.add)
+                act(B("xs", max(lo, LO), hi), V(X, max(lo, LO), hi), ACT.Identity, -2047.75)
+                ts(B("mq", lo, hi), B("pp", lo, hi), M12, M12, A.add, A.subtract)
+                mm([(Z, V("idf"), B("pp", lo, hi), True, False)])
+                mm([(Z, V("idn"), B("mq", lo, hi), False, True)])
+                act(B("sq", lo, hi), Z, ACT.Square, 511.875, 0.25)
+                tt(B("si", lo, hi), V(X, lo, hi), B("sq", lo, hi), A.add)
+                ts(B("hi", lo, hi), B("si", lo, hi), W - 1, None, A.bitwise_and)
+                cp(B("ho", lo - LO + 1, hi - LO + 1), B("hi", lo, hi))
+            for lo, hi, X in rng:
+                if not last:
+                    ts(B("ev", max(lo, LO), hi), V(X, max(lo, LO), hi), M1, M1, A.add, A.subtract)
+                else:
+                    act(V(XL, 128 + max(lo, LO), 128 + hi), V(X, max(lo, LO), hi), ACT.Identity, -0.25, -1.0)
+            if not last:
+                mm([(V(XL, 128, 256), V("id2"), B("ev"), True, False), (V(XL, 128, 256), V("idn"), B("xs"), False, True)])
+                act(V("win", w1 + OWN, w1 + OWN + M), V(XL, 128, 256), ACT.Identity, 1.0 - W)
                 send("S", t + 1, s, V("win", w1 + OWN, w1 + OWN + M), V("win", w1 + STR, w1 + STR + M))
+                mm([(V(XL, 256, 360), V("idp"), B("xs", LO - 1, M - 1), True, False), (V(XL, 256, 359), V("idn"), B("xs", LO, M - 1), False, True)])
+            if ENG["pen"] == "v":
+                ts(B("pen"), B("xs", LO, M), 3000.0, None, A.is_gt)
             else:
-                act(B("y0"), B("va"), ACT.Identity, -1.5)
-            act(B("pen"), B("va", LO, M), ACT.Relu, 1.5, -1.0)
+                act(B("pen"), B("xs", LO, M), ACT.Relu, -float(W // 2))
             mm([(V(K, 0, 104), V("idp"), V("low"), True, False), (V(K, 0, 104), V("idb"), B("pen"), False, False)])
             for a, b, eng in CFG["FG"]:
-                gat(eng, B("R", 16 * a, 16 * b), V("bk"), B("ho", a, b))
+                gat(eng, B("R", 16 * a, 16 * b), V("bk", 0, W), B("ho", a, b))
             TL, at = CFG["TL"], 0
             for ti, (mode, a, b) in enumerate(TL):
                 j0, j1, o, wd, fin = 16 * (a - LO), 16 * (b - LO), V(K, a - LO, b - LO), b - a, ti + 1 == len(TL)
-                sel = lambda n, cl: V(n, 15 - cl, 143 - cl)
                 if mode == "max":
-                    tt(B("AB", at, at + 16 * wd), B("R", j0 + 16, j1 + 16), B("R", j0, j1), A.max)
+                    tt(B("AB", j0, j1), B("R", j0 + 16, j1 + 16), B("R", j0, j1), A.max)
                     mm([(o, sel("wn", cl), B("R", j0 + u + cl, j1 + u, 16), False, False) for cl in range(16) for u in (0, 16)])
-                    mm([(o, sel("w2", cl), B("AB", at + cl, at + 16 * wd, 16), False, fin and cl == 15) for cl in range(16)])
-                    at += 16 * wd
+                    mm([(o, sel("w2", cl), B("AB", j0 + cl, j1, 16), False, fin and cl == 15) for cl in range(16)])
                 elif mode == "row":
                     D = "D%d" % (tile[0] % ND)
                     tile[0] += 1
                     mm([(V(D, 0, j1 - j0), V("idp"), B("R", j0 + 16, j1 + 16), True, False), (V(D, 0, j1 - j0), V("idn"), B("R", j0, j1), False, True)])
-                    act(B("AB", at, at + 16 * wd), V(D, 0, j1 - j0), ACT.Abs)
-                    at += 16 * wd
+                    act(B("AB", j0, j1), V(D, 0, j1 - j0), ACT.Abs)
                 else:
-                    mm([(o, sel("wp", cl), B("AB", at - 16 * wd + cl, at, 16), False, fin and cl == 15) for cl in range(16)])
-            m_, q_ = B("sm", 0, 1), B("sm", 1, 2)
-            red(m_, V(K, 0, 104), A.max)
-            ts(q_, m_, M7, M7, A.add, A.subtract)
-            if t + 1 < RO:
-                nn = V("em", e0 + 2 * EM + 128, e0 + 2 * EM + 129)
-                ts(nn, q_, m_, 75.5, A.subtract, A.add)
-                ends(t + 1, s)
+                    mm([(o, sel("wp", cl), B("AB", j0 + cl, j1, 16), False, fin and cl == 15) for cl in range(16)])
+            if last:
+                ts(B("sm", 7, 8), B("ai", t, t + 1), B("ai", 0, 1), None, A.subtract)
+                ts(B("sq"), V("idf"), B("sm", 7, 8), None, A.mult)
+                mm([(V(XL, 256, 360), B("sq"), V("one"), True, False)])
+                mm([(V(XL, 256, 360), sel("w1", cl), B("R", 16 + cl, 1680, 16), False, cl == 15) for cl in range(16)])
+            red(B("sm", 0, 1), V(K, 0, 104), A.max, False, True)
+            if ENG["mq"] == "v":
+                ts(B("mc"), V(K, 0, 104), B("sm", 0, 1), None, A.add)
             else:
-                nn = V("yl", s, s + 1)
-                ts(nn, q_, m_, 75.5, A.subtract, A.add)
-                ts(B("mz"), V("iot", 0, M), nn, None, A.is_lt)
-                tt(V("yo", s, 256, 2), B("y0"), B("mz"), A.mult)
-            ts(B("orr", 0, 1), nn, 16.0, CLR, A.mult, A.add)
-            gat("a", B("gr"), B("R"), B("orr", 0, 1))
-            if t + 1 == RO:
-                gain(t, s)
-                act(V("yb", s, s + 1), B("ai", t + 1, t + 2), ACT.Identity, 2047.5)
+                act(B("mc"), V(K, 0, 104), ACT.Identity, B("sm", 0, 1))
+            if not last:
+                scan(B("rr"), B("mc"), V(XL, 256, 360), -1e9, A.max)
+                scan(V("em", e0 + 2 * EM - 104, e0 + 2 * EM), B("mc"), V("cm"), -1e4, A.max)
+                ends(t + 1, s, B("rr", 103, 104))
+            else:
+                scan(B("rr"), B("mc"), V("cz"), -1.0, A.max)
+                tt(V("yo", 2 * LO + s, 256, 2), V(XL, 128 + LO, 256), B("rr"), A.mult)
+                tt(B("pp", 0, 104), V(XL, 256, 360), B("mc"), A.add)
+                red(V("yb", s, s + 1), B("pp", 0, 104), A.max)
+                scan(V("yl", s, 208, 2), B("mc"), V("dl"), -1e4, A.max)
     add("s", "store", ("ys", V("yo")), [V("yo")], [], 60.0, 2200.0)
-    add("s", "store", ("yn", V("yl")), [V("yl")], [], 60.0, 2000.0)
+    add("s", "store", ("yn", V("yl", 206, 208)), [V("yl")], [], 60.0, 2000.0)
     add("a", "store", ("ya", V("yb")), [V("yb")], [], 60.0, 2000.0)
     return ops
 
@@ -281,7 +320,9 @@ def link(ops):
                 same = ops[j]["eng"] == o["eng"] and ops[j]["kind"] not in ("load", "send") and o["kind"] not in ("store", "send")
                 hit = lo < v[2] and v[1] < hi
                 if ps:
-                    need = (not same) or (hit and w and not wr)
+                    need = (not same) or (hit and (w or wr))
+                    if same and not need and o["eng"] != "p":
+                        continue
                 elif hit and (w or wr):
                     need = True
                 else:
@@ -335,16 +376,76 @@ def order(ops, bias):
     return sorted(out, key=lambda i: (start[i], pos[i])), start, end
 
 
-def replay(ops, seq, case):
-    cost, lat, sem = case
-    free, end = {}, [0.0] * len(ops)
-    for i in seq:
-        e = ops[i]["eng"]
-        at = max([free.get(e, 0.0)] + [end[j] + sem if w else end[j] for j, w in ops[i]["deps"].items() if w or not e])
-        if e:
-            free[e] = at + cost[i]
-        end[i] = at + cost[i] + lat[i]
-    return max(end)
+def improve(ops, seq, cases):
+    n, ids, anc, wait, tags = len(ops), {}, [0] * len(ops), [], {}
+    eng = [ids.setdefault(o["eng"] or i, len(ids)) for i, o in enumerate(ops)]
+    for i, o in enumerate(ops):
+        keep = []
+        for j in sorted([j for j, w in o["deps"].items() if w], reverse=True):
+            if not anc[i] >> j & 1:
+                keep.append(j)
+                anc[i] |= anc[j] | 1 << j
+        wait.append(keep)
+        tags.setdefault(o.get("tag", i), []).append(i)
+    deps, succ = [list(o["deps"]) for o in ops], [o["succ"] for o in ops]
+    arr = [-1 if o["eng"] else o["after"][0] for o in ops]
+    (c0, l0, s0), (c1, l1, s1), (c2, l2, s2) = cases
+    r0, r1, r2 = [0.0] * n, [0.0] * n, [0.0] * n
+
+    def replay(seq):
+        f0, f1, f2 = [0.0] * len(ids), [0.0] * len(ids), [0.0] * len(ids)
+        for i in seq:
+            e, j = eng[i], arr[i]
+            a0, a1, a2 = (r0[j] - s0, r1[j] - s1, r2[j] - s2) if j >= 0 else (f0[e], f1[e], f2[e])
+            for j in wait[i]:
+                if r0[j] > a0:
+                    a0 = r0[j]
+                if r1[j] > a1:
+                    a1 = r1[j]
+                if r2[j] > a2:
+                    a2 = r2[j]
+            f0[e], f1[e], f2[e] = a0 + c0[i], a1 + c1[i], a2 + c2[i]
+            r0[i], r1[i], r2[i] = f0[e] + l0[i] + s0, f1[e] + l1[i] + s1, f2[e] + l2[i] + s2
+        ends = (max(r0), max(r1), max(r2))
+        return ends[0] + ends[1] + 0.8 * ends[2] + 0.5 * (sum(r0) + sum(r1) + 0.8 * sum(r2)) / n, ends
+
+    def move(seq, p, k):
+        i, q, left = seq[p], p, abs(k)
+        while left:
+            q += 1 if k > 0 else -1
+            if not 0 <= q < n:
+                return None
+            left -= eng[seq[q]] == eng[i]
+        rel = succ if k > 0 else deps
+        need, engs, take, rest = set(rel[i]), set(), [i], []
+        for x in (seq[p + 1:q + 1] if k > 0 else seq[q:p][::-1]):
+            if x in need or eng[x] in engs:
+                if eng[x] == eng[i]:
+                    return None
+                take.append(x)
+                need.update(rel[x])
+                engs.add(eng[x])
+            else:
+                rest.append(x)
+        return seq[:p] + rest + take + seq[q + 1:] if k > 0 else seq[:q] + take[::-1] + rest[::-1] + seq[p + 1:]
+
+    rs, steps = np.random.RandomState(CFG["seed"]), CFG["steps"]
+    free = [i for i, o in enumerate(ops) if o["eng"] and o["kind"] != "load"]
+    pick, ks = rs.randint(0, len(free), steps), rs.choice([-6, -3, -2, -1, -1, -1, 1, 1, 1, 2, 3, 6], steps)
+    every, slack = rs.rand(steps) < 0.5, rs.exponential(size=steps) * CFG["temp"]
+    now, ends = replay(seq)
+    best = (now, ends, seq)
+    for it in range(steps):
+        i, new = free[pick[it]], seq
+        for x in (tags[ops[i].get("tag", i)] if every[it] else [i]):
+            new = move(new, new.index(x), int(ks[it])) or new
+        if new is not seq:
+            val, ends = replay(new)
+            if val <= now + slack[it] * (1 - it / steps):
+                now, seq = val, new
+                if val < best[0]:
+                    best = (val, ends, new)
+    return best
 
 
 PLAN = []
@@ -360,29 +461,12 @@ def plan():
             CFG.update(keep)
         ops = build()
         link(ops)
-        rs = np.random.RandomState(CFG["seed"])
         bias = [-CFG["lag"] * o["s"] for o in ops]
         for i, o in enumerate(ops):
             if o["kind"] == "load":
                 bias[i] = 1e6 * (20 - i)
-        per = [i for i, o in enumerate(ops) if o["kind"] == "scan" and o["args"][4] == A.add]
-        per = per[NCH] - per[0]
-        now, best = 1e30, None
-        for it in range(CFG["tries"] + 1):
-            b2 = list(bias)
-            at, wide, step = int(rs.randint(5, len(ops))), int(rs.choice([1, 2, 4, 8, 16, 40])), int(rs.choice([len(ops), 2 * per, per]))
-            amount = float(rs.normal()) * float(rs.choice([300.0, 1000.0, 3000.0])) * (it > 0)
-            for j in range(at % step, len(ops), step):
-                for i in range(j, min(j + wide, len(ops))):
-                    b2[i] += amount
-            got = order(ops, b2)
-            all_ = [replay(ops, got[0], c) for c in cases]
-            val = sum(all_) / len(all_)
-            if val <= now + CFG["temp"] * (1 - it / (CFG["tries"] + 1)) * float(rs.exponential()):
-                now, bias = val, b2
-                if best is None or now < best[3]:
-                    best = got + (val, all_)
-        PLAN.append((ops,) + best)
+        best = improve(ops, order(ops, bias)[0], cases)
+        PLAN.append((ops, best[2], best[1], cases))
     return PLAN[0]
 
 
@@ -444,13 +528,13 @@ def rank_program(g, core, T, topo):
         elif kind == "cp":
             ins = q.tensor_copy(ap(x[0]), ap(x[1]))
         elif kind == "red":
-            ins = q.tensor_reduce(ap(x[0]), ap(x[1]), AxisListType.X, x[2], apply_absolute_value=x[3])
+            ins = q.tensor_reduce(ap(x[0]), ap(x[1]), AxisListType.X, x[2], negate=x[4], apply_absolute_value=x[3])
         elif kind == "fill":
             ins = q.memset(ap(x[0]), x[1])
         elif kind == "scan":
             ins = q.tensor_tensor_scan(ap(x[0]), ap(x[1]), ap(x[2]), ap(x[3]), x[4], A.add)
         elif kind == "act":
-            ins = q.activation(ap(x[0]), ap(x[1]), x[2], bias=ap(x[3]), scale=ap(x[4]))
+            ins = q.activation(ap(x[0]), ap(x[1]), x[2], bias=ap(x[3]), scale=ap(x[4]), accum_out=ap(x[5]))
         elif kind == "gat":
             src = ap(x[1]).indirect(ap(x[2]))
             if e == "a":

@@ -3,41 +3,44 @@ from concourse.mybir import AluOpType, AxisListType, ActivationFunctionType
 
 RO, M, LO, W, NR = 5, 128, 24, 4096, 8
 CFG = {
-    "KC": [24, 128],
-    "DG": [24, 76, 128],
-    "SG": [(24, 50, "a"), (50, 76, "v"), (76, 102, "a"), (102, 128, "v")],
-    "FG": [(0, 20, "v"), (20, 72, "a"), (72, 90, "v"), (90, 105, "v")],
-    "TL": [("row", 24, 43), ("row", 43, 69), ("sum", 24, 69), ("row", 69, 95), ("row", 95, 113), ("row", 113, 128), ("sum", 69, 128)],
-    "eng": {"mq": "v", "pen": "v", "E": "v", "gr": "a", "dcl": "a"},
-    "cyc": 0.9, "pe": 0.45, "gat": 1.5, "tt2": 1.0, "sem": 160.0, "issue": 600.0, "land": 2600.0, "fix": 90.0, "vfix": 50.0, "peu": 400,
-    "first": 1200.0, "lag": 2000.0, "seed": 3, "steps": 30000, "temp": 30.0,
-    "cases": [{"cyc": 0.83, "pe": 0.42, "sem": 170.0, "fix": 70.0, "vfix": 40.0}, {"cyc": 0.83, "pe": 0.42, "sem": 110.0, "fix": 150.0, "vfix": 80.0},
-              {"cyc": 1.15, "pe": 0.58, "gat": 1.7, "sem": 170.0, "fix": 70.0, "vfix": 40.0, "land": 2800.0, "tt2": 2.0}],
+    "SG": [[(0, 26, "a"), (26, 52, "v")],
+           [(0, 30, "a"), (30, 42, "v"), (42, 52, "v")]],
+    "RC": [[(0, 258, "a")], [(0, 258, "a")]],
+    "FG": [[(0, 20, "v"), (20, 62, "a"), (62, 84, "v"), (84, 105, "v")], [(0, 20, "v"), (20, 62, "a"), (62, 84, "v"), (84, 94, "v"), (94, 105, "v")],
+           [(0, 20, "v"), (20, 62, "a"), (62, 84, "v"), (84, 105, "v")]],
+    "TL": [[("row", 24, 43), ("row", 43, 64), ("sum", 24, 64), ("row", 64, 85), ("row", 85, 107), ("row", 107, 128), ("sum", 64, 128)]] * 3,
+    "eng": {"mq": "v", "pen": "v", "E": "v", "gr": "a", "dcl": 4, "hq": "v", "fc": "v", "gain": "a", "z": "v", "lin": "vvvaavvvaaav"}, "both": 1,
+    "cyc": 0.9, "pe": 0.55, "gat": 1.4, "tt2": 2.0, "sem": 160.0, "issue": 600.0, "land": 2200.0, "fix": 90.0, "vfix": 50.0, "peu": 400,
+    "first": 1200.0, "lag": 2000.0, "seed": 3, "steps": 50000, "temp": 300.0, "aim": 0.8, "turns": 1, "tries": 600, "warm": 600.0,
+    "cases": [{"cyc": 0.83, "pe": 0.52, "gat": 1.15, "sem": 150.0, "fix": 70.0, "vfix": 40.0, "land": 1900.0, "issue": 400.0},
+              {"cyc": 0.9, "pe": 0.5, "gat": 1.6, "sem": 110.0, "fix": 120.0, "vfix": 60.0, "land": 2300.0},
+              {"cyc": 1.2, "pe": 0.75, "gat": 1.5, "sem": 170.0, "fix": 100.0, "vfix": 60.0, "land": 2800.0}],
 }
-NCH = len(CFG["KC"]) - 1
-REG, OWN, STR = 424, 88, 296
-EM, EE, EL = 240, 112, 136
+REG, OWN, STR = 840, 168, 584
+EM, EE, ES = 288, 112, 153
+EL, LE, LS = 192, 8, 49
+EB, FX, DX = 32, 232, 128
 F32, BF, F16, I32, U16 = "float32", "bfloat16", "float16", "int32", "uint16"
 SCRATCH = {}
-for _n, _c, _d in (("bk", W + 16, BF), ("ar", 256, I32), ("ln", 4, I32), ("ti", 4, I32), ("win", REG * 2 * RO, F32), ("em", EM * 2 * RO, BF),
-                   ("el", EL * 2 * RO, BF), ("thf", 2, F32), ("ea", 256, I32), ("iot", 144, BF), ("low", 104, BF), ("pmi", 128, BF),
-                   ("blk", 128, BF), ("bm", 128, BF), ("pid", 2, I32), ("pc", 8, F32), ("idp", 128, BF), ("idn", 128, BF), ("id2", 128, BF),
-                   ("idb", 128, BF), ("idf", 128, F32), ("one", 104, F32), ("dcl", 2048, BF), ("wp", 144, BF), ("w2", 144, BF),
-                   ("wn", 144, BF), ("w1", 144, BF), ("dg", 16, F32), ("fp", 16, BF), ("fn", 16, BF), ("od", 18, BF), ("cd", 18, BF),
-                   ("cc", 128, BF), ("cq", 128, F32), ("cm", 104, F32), ("dl", 104, F32), ("cz", 104, F32), ("bo", 8, F32),
-                   ("yo", 256, F32), ("yl", 208, F32), ("yb", 2, F32)):
+for _n, _c, _d in (("bk", W + 16, BF), ("ar", 256, I32), ("ln", 4, I32), ("ti", 4, I32), ("win", REG * 2, F32), ("em", EM * 2 * RO, F16),
+                   ("el", EL * 2 * RO, F16), ("thf", 2, F32), ("kk", 104, BF), ("iot", 144, BF), ("low", 104, BF), ("pmi", 128, BF),
+                   ("blk", 128, BF), ("bm", 128, BF), ("pid", 4, I32), ("b8", 8, F32), ("pc", 12, F32), ("idp", 128, BF), ("idn", 128, BF), ("id2", 128, BF),
+                   ("idb", 128, BF), ("idw", 128, BF), ("idf", 128, F32), ("tg", 128, F32), ("dn", 128, BF), ("dx", 104, F16),
+                   ("Gx", 832, F16), ("xo", 104, F16), ("ofx", 52, U16), ("one", 104, F32), ("dcl", 2052, BF), ("wp", 144, BF), ("w2", 144, BF),
+                   ("wn", 144, BF), ("w1", 144, BF), ("dg", 16, F32), ("fp", 16, F16), ("fn", 16, F16), ("od", 18, BF), ("cd", 18, F16),
+                   ("cc", 128, BF), ("cq", 128, BF), ("cm", 104, BF), ("dl", 104, F32), ("cz", 104, F32), ("bo", 8, F32), ("rp", 260, BF),
+                   ("onb", 128, BF), ("yo", 256, F32), ("yl", 208, F32), ("yb", 2, F32)):
     SCRATCH[_n] = ("sbuf", [128, _c], _d)
 for _s in range(2):
-    for _n, _c, _d in (("pp", 128, F32), ("sq", 128, F32), ("y0", 128, F32), ("xs", 128, F16), ("ev", 128, F16), ("mq", 128, BF),
+    for _n, _c, _d in (("pp", 128, F32), ("sq", 128, F32), ("y0", 128, F32), ("xs", 128, F16), ("ev", 128, F16), ("mq", 128, F16),
                        ("mc", 104, F32), ("rr", 104, F32), ("si", 128, I32), ("hi", 128, I32), ("ho", 106, U16), ("R", 1680, BF),
-                       ("AB", 1664, BF), ("G", 1664, F16), ("xm", 128, F16), ("mz", 104, F16), ("off", 104, U16), ("pen", 104, BF),
-                       ("nc", 104, BF), ("sm", 16, F32), ("ai", 8, F32), ("oq", 2, U16), ("orr", 2, U16), ("l8", 8, U16),
+                       ("AB", 1664, BF), ("G", 832, F16), ("xm", 128, F16), ("mz", 128, F16), ("off", 52, U16), ("pen", 104, BF),
+                       ("nc", 104, F16), ("nz", 104, F16), ("yy", 52, F16), ("sm", 16, F32), ("ai", 8, F32), ("oq", 2, U16), ("orr", 2, U16), ("l8", 8, U16),
                        ("gq", 18, F32), ("gr", 16, BF)):
         SCRATCH["%s%d" % (_n, _s)] = ("sbuf", [128, _c], _d)
     SCRATCH["K%d" % _s] = ("psum", [128, 512], F32)
-    for _c in range(NCH):
-        SCRATCH["X%d%d" % (_s, _c)] = ("psum", [128, 512], F32)
-ND = 6 - 2 * NCH
+    SCRATCH["X%d" % _s] = ("psum", [128, 512], F32)
+ND = 4
 for _c in range(ND):
     SCRATCH["D%d" % _c] = ("psum", [128, 512], F32)
 SEMAPHORES = (["cv", "ca", "cp", "cg", "sent"] + ["d%d" % i for i in range(10)]
@@ -104,20 +107,29 @@ def build():
         while lst:
             k, c = 0, 0
             while k < len(lst) and (c < CFG["peu"] or k % 2):
-                k, c = k + 1, c + max(64, cols(lst[k][2])) * (4 if SCRATCH[lst[k][2][0]][2] == F32 else 1)
+                k, c = k + 1, c + max(min(64, cols(lst[k][1])), cols(lst[k][2])) * (4 if SCRATCH[lst[k][2][0]][2] == F32 else 1)
             add("p", "mm", lst[:k], [x[1] for x in lst[:k]] + [x[2] for x in lst[:k]], [x[0] for x in lst[:k]], c * CFG["pe"], 60.0)
             lst = lst[k:]
 
-    def iota(out, pattern, base, ch):
-        add("g", "iota", (out, pattern, base, ch), [], [out], 130 + 2 * cols(out) * cyc)
+    def iota(out, pattern, base, ch, after=()):
+        add("g", "iota", (out, pattern, base, ch), [], [out], 130 + 2 * cols(out) * cyc, after=after)
+
+    def const(out, c, after=()):
+        iota(out, [[0, cols(out)]], int(c), 0, after)
+
+    def lin(eng, out, in0, scale, bias):
+        if eng == "v":
+            ts(out, in0, scale, bias, A.mult, A.add)
+        else:
+            act(out, in0, ACT.Identity, bias, scale)
 
     def load(eng, out, name, lo, hi, lat):
-        add(eng, "load", (out, name, lo, hi), [], [out], 60.0, lat)
+        add(eng, "load", (out, name, lo, hi), [], [out], 60.0, lat, [i for i, o in enumerate(ops) if o["eng"] == eng])
 
     def send(kind, t, s, src, dst):
         sent.append(add("g", "send", (kind, t, s, src, dst), [src], [], CFG["issue"] + (0 if sent else CFG["first"]), after=sent[:1]))
         i = sent[-1]
-        add(None, "arr", "a%s%d%d" % (kind, t, s), [], [dst], 0.0, CFG["land"] + (500 if kind == "S" else 0), after=[i])
+        add(None, "arr", "a%s%d%d" % (kind, t, s), [], [dst], 0.0, CFG["land"] + 2 * cols(src), after=[i])
 
     load("s", V("ar"), "arms", 0, 256, 2200.0)
     load("a", V("ln", 0, 2), "len0", 0, 2, 2000.0)
@@ -136,140 +148,196 @@ def build():
     ts(CLR, CL, 16.0 * (M - LO + 1), None, A.add)
     ts(V("dg"), V("iot", 0, 16), CL, None, A.is_equal)
     ts(V("bm"), V("blk"), P16, None, A.is_equal)
-    ts(V("bo"), V("bm", 0, 128, 16), -GAP, GAP + W // 2, A.mult, A.add)
-    fill(V("bk", W, W + 16), 0.0)
-    fill(V("cq"), 0.25)
-    fill(V("cm"), -1.0)
-    fill(V("em", EE - 2, 2 * EM, EM), 0.0)
+    ts(V("pid", 2, 3), V("pid", 0, 1), EB - 16, None, A.bitwise_and)
+    cp(V("pc", 6, 7), V("pid", 2, 3))
+    ts(V("b8"), V("iot", 0, 8), 16.0, V("pc", 6, 7), A.mult, A.is_equal)
+    ts(V("bo"), V("b8"), -GAP, GAP + W // 2, A.mult, A.add)
     ts(V("fp"), V("iot", 0, 16), CL, None, A.is_equal)
-    ts(V("fn"), V("iot", 0, 16), CL, -1.0, A.is_equal, A.mult)
-    ts(V("pc", 4, 5), V("dg", 0, 1), W // 2, None, A.mult)
-    ts(V("pc", 5, 6), V("dg", 1, 2), -0.25, V("pc", 4, 5), A.mult, A.add)
-    ts(V("cc"), V("iot", 0, 128), 0.0, V("pc", 5, 6), A.mult, A.add)
-    fill(V("cd", 0, 16), 0.0)
-    fill(V("cd", 16, 17), float(M + OWN))
-    fill(V("cd", 17, 18), float(STR - OWN))
-    ts(V("od"), V("iot", 0, 18), CL, -GAP, A.not_equal, A.mult)
-    fill(V("od", 16, 18), 0.0)
-    ts(V("low"), V("iot", LO, M), -GAP, None, A.mult)
-    for name, c in (("idp", 1.0), ("idn", -1.0), ("id2", 2.0), ("idb", -2.0 ** (33 if ENG["pen"] == "v" else 22)), ("idf", 1.0)):
-        ts(V(name), V("pmi"), 0.0, c, A.is_equal, A.mult)
-    for name, c in (("wp", 128 * GAP), ("w2", 256 * GAP), ("wn", -128 * GAP), ("w1", 1.0)):
-        if name in ("wp", "w1") or any(x[0] == "max" for x in CFG["TL"]):
-            ts(V(name), V("iot"), P15, c, A.is_equal, A.mult)
+    ts(V("od", 0, 16), V("iot", 0, 16), CL, -GAP, A.not_equal, A.mult)
+    ts(V("idp"), V("pmi"), 0.0, None, A.is_equal)
+    ts(V("wp"), V("iot"), P15, 128 * GAP, A.is_equal, A.mult)
+    ts(V("pid", 3, 4), V("pid", 0, 1), 1, None, A.bitwise_and)
+    ODD, EVEN, BASE = V("pc", 7, 8), V("pc", 8, 9), V("pc", 9, 10)
+    cp(ODD, V("pid", 3, 4))
+    lin("v", EVEN, ODD, -1.0, 1.0)
+    lin("v", BASE, ODD, 1.0, float(OWN))
+    for out, c in ((V("win", 0, REG * 2, REG), 0), (V("bk", W, W + 16), 0), (V("cm"), -2), (V("od", 16, 17), 0), (V("dcl", 0, 2), 0),
+                   (V("dcl", 2050, 2052), 0), (V("rp", 0, 260, 130), 0), (V("rp", 129, 260, 130), 0)):
+        const(out, c)
+    for i in range(2):
+        const(V("win", REG * i + 8, REG * i + OWN - 2), MARK)
+        const(V("win", REG * i + OWN + 2 * M, REG * i + STR - 2), MARK)
+    for c, x in ((ES - 1, MARK), (ES + M, 0.0), (EE - 2, 0.0), (ES - 3, 0.0)):
+        lin("v", V("em", c, EM * 2 * RO, EM), V("iot", 0, 2 * RO), 0.0, x)
+    lin("a", V("cd", 0, 16), V("iot", 0, 16), 0.0, 0.0)
+    lin("a", V("cd", 16, 17), BASE, 1.0, 2.0 * M)
+    lin("a", V("cd", 17, 18), BASE, 0.0, float(STR - OWN))
+    lin("v", V("rp", 1, 129), V("idp"), EVEN, 0.0)
+    lin("v", V("rp", 131, 259), V("idp"), ODD, 0.0)
+    e = iter(ENG["lin"])
+    lin(next(e), V("pc", 4, 5), V("dg", 0, 1), W / 2, 0.0)
+    lin(next(e), V("pc", 5, 6), V("dg", 1, 2), -0.25, V("pc", 4, 5))
+    lin(next(e), V("cc"), V("iot", 0, 128), 0.0, V("pc", 5, 6))
+    lin(next(e), V("cq"), V("iot", 0, 128), 0.0, 0.25)
+    lin(next(e), V("low"), V("iot", LO, M), -GAP, 0.0)
+    lin(next(e), V("kk"), V("iot", LO, M), 2.0, -2.0 * M)
+    lin(next(e), V("fn"), V("fp"), -1.0, 0.0)
+    for name, c in (("idn", -1.0), ("id2", 2.0), ("idw", -float(W)), ("idb", -2.0 ** (33 if ENG["pen"] == "v" else 22)), ("idf", 1.0)):
+        lin(next(e), V(name), V("idp"), c, 0.0)
+    for name, c in (("w1", 2.0 ** -20), ("w2", 2.0), ("wn", -1.0)):
+        if name == "w1" or any(x[0] == "max" for y in CFG["TL"] for x in y):
+            lin("a", V(name), V("wp"), c, 0.0)
     for cl in range(16):
-        if ENG["dcl"] == "a":
-            act(V("dcl", 128 * cl, 128 * cl + 128), V("idp"), ACT.Copy, 0.0, V("dg", cl, cl + 1))
-        else:
-            ts(V("dcl", 128 * cl, 128 * cl + 128), V("idp"), V("dg", cl, cl + 1), None, A.mult)
+        lin("v" if cl < ENG["dcl"] else "a", V("dcl", 128 * cl + 2, 128 * cl + 130), V("idp"), V("dg", cl, cl + 1), 0.0)
     cp(V("thf"), V("ti", 0, 2))
-    ts(V("ea"), V("ar"), W - 2, None, A.bitwise_and)
-    cp(V("yo", 0, 2 * LO), V("ar", 0, 2 * LO))
-    fill(V("win", 0, REG * 2 * RO, REG), 0.0)
-    for i in range(2 * RO):
-        for a in (OWN, STR):
-            if i < 2:
-                fill(V("win", REG * i + a - 80, REG * i + a), MARK)
-            else:
-                iota(V("win", REG * i + a - 80, REG * i + a), [[0, 80]], int(MARK), 0)
-    iota(V("one"), [[0, 104]], 1, 0)
-    iota(V("cz"), [[0, 104]], 0, 0)
-    iota(V("dl", 0, 103), [[0, 103]], -1, 0)
-    iota(V("dl", 103, 104), [[0, 1]], M - 1, 0)
 
     def ends(t, s, code):
-        e0, l0 = EM * (2 * t + s) + EE, EL * (2 * t + s) + 8
-        ts(V("l8%d" % s), V("bo"), code, float(W), A.add, A.min)
-        gat(ENG["E"], V("em", e0, e0 + 128), V("bk"), V("l8%d" % s))
-        send("E", t, s, V("em", e0 - 2, e0 + 128), V("el", l0 - 2, l0 + 128))
+        e0, l0 = EM * (2 * t + s) + EE, EL * (2 * t + s) + LE
+        ts(V("l8%d" % s, 0, EB // 16), V("bo", 0, EB // 16), code, float(W), A.add, A.min)
+        gat(ENG["E"], V("em", e0, e0 + EB), V("bk"), V("l8%d" % s, 0, EB // 16))
+        send("E", t, s, V("em", e0 - 2, e0 + EB), V("el", l0 - 2, l0 + EB))
+
+    def codes(t, s):
+        c0, l0, more = EM * (2 * t + s) + ES, EL * (2 * t + s) + LS, 1 if t else 3
+        send("S", t, s, V("em", c0 - more, c0 + M + 1), V("el", l0 - more, l0 + M + 1))
+
+    def lanes(s, name, c0, who):
+        X, w0 = "X%d" % s, REG * s + (OWN, STR)[who] - 2
+        mm([(V(X, FX + ch, FX + 258, 2), V("rp", 130 * ch + 1 + ch - i, 130 * ch + 129 + ch - i), V(name, c0 - i, c0 - i + M + 1), i == 0, i == 1)
+            for ch in range(2) for i in range(2)])
+        for a, b, eng in CFG["RC"][who]:
+            if eng == "a":
+                act(V("win", w0 + a, w0 + b), V(X, FX + a, FX + b), ACT.Copy)
+            else:
+                cp(V("win", w0 + a, w0 + b), V(X, FX + a, FX + b))
+
+    def diagonal(out, G, i, alone):
+        mm([(out, V("dcl", 128 * (c // 2 * 2 + i) + 2 + i - c % 2, 128 * (c // 2 * 2 + i) + 130 + i - c % 2), V(G, c, 832, 16),
+             alone and c == 0, alone and c == 15) for c in range(16)])
+
+    def turn(out, src, pick, stop):
+        return [(out + (p, p + EB), src + (p, p + EB), pick + (p, p + EB), False, stop) for p in range(0, 128, EB)]
 
     for s in range(2):
         B = lambda n, lo=0, hi=None, st=1: V("%s%d" % (n, s), lo, hi, st)
-        w0, cur[0] = REG * s, s
-        n_ = V("em", EM * s + EE - 1, EM * s + EE)
+        cur[0] = s
+        n_ = B("sm", 8, 9)
         ts(B("xs"), V("ar", s, 256, 2), -float(W // 2), None, A.add)
-        ts(B("pp"), V("ea", s, 256, 2), 2.0, 1.0 - W, A.mult, A.add)
-        tt(V("win", w0 + OWN, w0 + OWN + M), B("pp"), B("xs"), A.subtract)
-        send("S", 0, s, V("win", w0 + OWN, w0 + OWN + M), V("win", w0 + STR, w0 + STR + M))
+        ts(B("si"), V("ar", s, 256, 2), W - 2, None, A.bitwise_and)
+        ts(B("X", 0, M), B("si"), 2.0, 1.0 - W, A.mult, A.add)
+        tt(V("em", EM * s + ES, EM * s + ES + M), B("X", 0, M), B("xs"), A.subtract)
         act(B("y0"), B("xs"), ACT.Copy)
-        ts(n_, V("ln", s, s + 1), -float(M), None, A.add)
+        for out in (V("em", EM * s + ES - 2, EM * s + ES - 1), n_, V("em", EM * s + EE - 1, EM * s + EE)):
+            ts(out, V("ln", s, s + 1), 2.0, -2.0 * M, A.mult, A.add)
+        codes(0, s)
         ts(B("oq", 0, 1), V("ln", s, s + 1), -1.0, None, A.add)
         gat("v", B("gq", 0, 16), B("y0"), B("oq", 0, 1), V("dg"))
         red(B("sm", 2, 3), B("gq", 0, 16), A.add)
         ends(0, s, B("sm", 2, 3))
-        cp(B("ev", 0, LO), V("ea", s, 2 * LO, 2))
-        cp(B("xm", LO - 1, LO), B("xs", LO - 1, LO))
-        red(B("sm", 6, 7), B("y0", 0, LO - 1), A.add)
-        ts(B("ai", 0, 1), B("sm", 6, 7), (LO - 1) * (W // 2) + 2048.5, None, A.add)
-        ts(B("rr"), V("low"), 1.0 / GAP, n_, A.mult, A.add)
-        ts(B("mc"), B("rr"), -float(M), -GAP, A.is_gt, A.mult)
-        ts(B("rr"), B("rr"), float(M - 1), None, A.add)
-        tt(B("nc"), B("rr"), B("mc"), A.add)
+        act(B("ev", 0, LO), B("X", 0, LO), ACT.Identity, -0.5, 0.5)
+        act(B("xm", LO - 1, LO), B("xs", LO - 1, LO), ACT.Copy)
+        act(B("sq", 0, LO - 1), B("xs", 0, LO - 1), ACT.Copy, acc=B("sm", 6, 7))
+        act(B("ai", 0, 1), B("sm", 6, 7), ACT.Identity, (LO - 1) * (W // 2) + 2048.5)
+        act(V("yo", s, 2 * LO, 2), B("xs", 0, LO), ACT.Identity, W / 2)
+        ts(B("pen"), V("kk"), n_, -GAP, A.not_equal, A.mult)
+        scan(B("nc"), B("pen"), V("cm"), -1e4, A.max)
+    for out, c in ((V("one"), 1), (V("cz"), 0), (V("dl", 0, 103), -1), (V("dl", 103, 104), M - 1)):
+        const(out, c, sent[-1:])
 
-    KC = CFG["KC"]
     tile = [0]
     for t in range(RO):
         for s in range(2):
             B = lambda n, lo=0, hi=None, st=1: V("%s%d" % (n, s), lo, hi, st)
-            e0, l0, w0, w1 = EM * (2 * t + s) + EE, EL * (2 * t + s) + 8, REG * (2 * t + s), REG * (2 * t + 2 + s)
+            e0, l0, w0 = EM * (2 * t + s) + EE, EL * (2 * t + s) + LE, REG * s
             n_, n2 = V("em", e0 - 1, e0), V("el", l0 - 1, l0)
             nc = V("em", e0 - 104, e0) if t else B("nc")
-            K, last = "K%d" % s, t + 1 == RO
+            odd, even = (nc[0], nc[1] + 1, nc[2], 2), (nc[0], nc[1], nc[2], 2)
+            K, X, last = "K%d" % s, "X%d" % s, t + 1 == RO
+            both = t == 0 and s < CFG["both"]
             cur[:] = [s, {}]
-            rng = [(LO - 1 if c == 0 else KC[c], KC[c + 1], "X%d%d" % (s, c)) for c in range(NCH)]
-            XL = rng[-1][2]
             sel = lambda n, cl: V(n, 15 - cl, 143 - cl)
-            ts(B("mz"), nc, -1000.0, None, A.is_lt)
-            tt(B("xm", LO, M), B("xs", LO, M), B("mz"), A.mult)
+            ts(B("mz", LO, M), nc, -1000.0, None, A.is_lt)
+            tt(B("xm", LO, M), V(X, 0, 104) if t else B("xs", LO, M), B("mz", LO, M), A.mult)
+            lanes(s, "em", e0 - EE + ES, 0)
+            lanes(s, "el", l0 - LE + LS, 1)
             if t:
-                ts(B("orr", 0, 1), n_, 16.0, CLR, A.mult, A.add)
+                ts(B("orr", 0, 1), n_, 8.0, CLR, A.mult, A.add)
                 gat(ENG["gr"], B("gr"), B("R"), B("orr", 0, 1))
-                mm([(V(K, 104, 121), V("idp"), V("od", 0, 17), True, False), (V(K, 120, 121), V("idf"), B("ai", t - 1, t), False, False),
-                    (V(K, 104, 120), V("bm"), B("gr"), False, True)])
-                act(B("gq", 0, 17), V(K, 104, 121), ACT.Relu, acc=B("ai", t, t + 1))
-            mm([(V(K, 128, 146), V("idp"), V("cd"), True, False), (V(K, 144, 145), V("idp"), n_, False, False),
-                (V(K, 145, 146), V("idn"), n_, False, False), (V(K, 128, 144), V("em", e0, e0 + 128), V("fp"), False, False)])
-            mm([(V(K, 145, 146), V("idp"), n2, False, False), (V(K, 128, 144), V("el", l0, l0 + 128), V("fn"), False, True)])
-            red(B("sm", 3, 4), V(K, 128, 144), A.add, True)
-            ts(B("sm", 5, 6), B("sm", 3, 4), V("thf", s, s + 1), V(K, 145, 146), A.is_lt, A.mult)
-            ts(B("off"), nc, B("sm", 5, 6), V(K, 144, 145), A.add, A.add)
-            for a, b, eng in CFG["SG"]:
-                gat(eng, B("G", 16 * (a - LO), 16 * (b - LO)), V("win", w0, w0 + REG), B("off", a - LO, b - LO))
-            for lo, hi, X in rng:
-                mm([(V(X, lo, hi), V("bm"), V("cc", lo, hi), True, False), (V(X, lo, hi), V("idp"), B("xm", lo, hi), False, False)])
-                for a, b in zip(CFG["DG"], CFG["DG"][1:]):
-                    if lo <= a < hi:
-                        mm([(V(X, a, b), V("dcl", 128 * cl, 128 * cl + 128), B("G", 16 * (a - LO) + cl, 16 * (b - LO), 16), False,
-                             cl == 15 and b == hi) for cl in range(16)])
-            for c, (lo, hi, X) in enumerate(rng):
-                Z = V(K, 160 + lo, 160 + hi)
-                scan(B("pp", lo, hi), V("cq", lo, hi), V(X, lo, hi), B("ai", t, t + 1) if c == 0 else B("pp", lo - 1, lo), A.add)
-                act(B("xs", max(lo, LO), hi), V(X, max(lo, LO), hi), ACT.Identity, -2047.75)
-                ts(B("mq", lo, hi), B("pp", lo, hi), M12, M12, A.add, A.subtract)
-                mm([(Z, V("idf"), B("pp", lo, hi), True, False)])
-                mm([(Z, V("idn"), B("mq", lo, hi), False, True)])
-                act(B("sq", lo, hi), Z, ACT.Square, 511.875, 0.25)
-                tt(B("si", lo, hi), V(X, lo, hi), B("sq", lo, hi), A.add)
-                ts(B("hi", lo, hi), B("si", lo, hi), W - 1, None, A.bitwise_and)
-                cp(B("ho", lo - LO + 1, hi - LO + 1), B("hi", lo, hi))
-            for lo, hi, X in rng:
-                if not last:
-                    ts(B("ev", max(lo, LO), hi), V(X, max(lo, LO), hi), M1, M1, A.add, A.subtract)
+                if ENG["gain"] == "p":
+                    mm([(V(K, 104, 121), V("idp"), V("od", 0, 17), True, False), (V(K, 120, 121), V("idf"), B("ai", t - 1, t), False, False),
+                        (V(K, 104, 120), V("bm"), B("gr"), False, True)])
+                    act(B("gq", 0, 17), V(K, 104, 121), ACT.Relu, acc=B("ai", t, t + 1))
                 else:
-                    act(V(XL, 128 + max(lo, LO), 128 + hi), V(X, max(lo, LO), hi), ACT.Identity, -0.25, -1.0)
+                    mm([(V(K, 104, 120), V("idp"), V("od", 0, 16), True, False), (V(K, 104, 120), V("bm"), B("gr"), False, True)])
+                    red(B("sm", 11, 12), V(K, 104, 120), A.max)
+                    lin(ENG["gain"], B("ai", t, t + 1), B("sm", 11, 12), 1.0, B("ai", t - 1, t))
+            mm([(V(K, 128, 146), V("idp"), V("cd"), True, False), (V(K, 144, 145), V("idp"), n_, False, False),
+                (V(K, 145, 146), V("idn"), n_, False, False)] + turn(V(K, 128, 144), V("em", e0, e0 + EB), V("fp"), False))
+            mm([(V(K, 145, 146), V("idp"), n2, False, False)] + turn(V(K, 128, 144), V("el", l0, l0 + EB), V("fn"), True))
+            red(B("sm", 3, 4), V(K, 128, 144), A.add, True)
+            if both:
+                ts(B("sm", 9, 10), B("sm", 8, 9), BASE, 2.0 * M, A.add, A.add)
+                ts(B("sm", 10, 11), V("el", l0 - LE + LS - 2, l0 - LE + LS - 1), BASE, 2.0 * M + STR - OWN, A.add, A.add)
+                for G, off, end, D, at in (("Gx", "ofx", STR - 2, "D0", 9), (B("G")[0], B("off")[0], REG, "D1", 10)):
+                    ts(V(off), odd, B("sm", at, at + 1), None, A.add)
+                    for a, b, eng in CFG["SG"][s]:
+                        gat(eng, V(G, 16 * a, 16 * b), V("win", w0, w0 + end), V(off, a, b))
+                    for i in range(2):
+                        diagonal(V(D, i, 104, 2), G, i, True)
+                ts(B("nz"), nc, -1000.0, -1.0, A.is_gt, A.mult)
+                tt(V("xo"), V("D0", 0, 104), B("nz"), A.mult)
+                ts(B("nz"), nc, -1000.0, None, A.is_gt)
+                tt(V("dx"), V("D1", 0, 104), B("nz"), A.mult)
+                ts(V("tg"), V("idf"), V("thf", s, s + 1), None, A.mult)
+                ts(V("dn"), V("tg"), B("sm", 3, 4), None, A.is_gt)
+            else:
+                ts(B("sm", 5, 6), B("sm", 3, 4), V("thf", s, s + 1), V(K, 145, 146), A.is_lt, A.mult)
+                ts(B("off"), odd, B("sm", 5, 6), V(K, 144, 145), A.add, A.add)
+                for a, b, eng in CFG["SG"][s]:
+                    gat(eng, B("G", 16 * a, 16 * b), V("win", w0, w0 + REG), B("off", a, b))
+            lo, hi = LO - 1, M
+            mm([(V(X, lo, hi), V("bm"), V("cc", lo, hi), True, False), (V(X, lo, hi), V("idp"), B("xm", lo, hi), False, False)])
+            if both:
+                mm([(V(X, LO, M), V("idn"), V("xo"), False, False)])
+                mm([(V(X, LO, M), V("dn"), V("xo"), False, False), (V(X, LO, M), V("dn"), V("dx"), False, True)])
+            else:
+                ts(B("nz", 0, 52), even, -1000.0, None, A.is_gt)
+                diagonal(V(K, 300, 352), B("G")[0], 0, True)
+                diagonal(V(X, LO + 1, M, 2), B("G")[0], 1, False)
+                tt(B("yy"), V(K, 300, 352), B("nz", 0, 52), A.mult)
+                mm([(V(X, LO, M, 2), V("idp"), B("yy"), False, True)])
+            Z = V(K, 160 + lo, 160 + hi)
+            scan(B("pp", lo, hi), V("cq", lo, hi), V(X, lo, hi), B("ai", t, t + 1), A.add)
+            act(B("xs", LO, M), V(X, LO, M), ACT.Identity, -2047.75)
+            if ENG["z"] == "p":
+                lin(ENG["hq"], B("mq", lo, hi), B("pp", lo, hi), 1.0 / W, 1024.0)
+                mm([(Z, V("idf"), B("pp", lo, hi), True, False)])
+                mm([(Z, V("idw"), B("mq", lo, hi), False, True)])
+                act(B("sq", lo, hi), Z, ACT.Square, 511.875 + 2.0 ** 20, 0.25)
+            else:
+                ts(Z, B("pp", lo, hi), M12, M12, A.add, A.subtract)
+                tt(B("y0", lo, hi), B("pp", lo, hi), Z, A.subtract)
+                act(B("sq", lo, hi), B("y0", lo, hi), ACT.Square, 511.875, 0.25)
+            tt(B("si", lo, hi), V(X, lo, hi), B("sq", lo, hi), A.add)
+            ts(B("hi", lo, hi), B("si", lo, hi), W - 1, None, A.bitwise_and)
+            cp(B("ho", 0, hi - lo), B("hi", lo, hi))
             if not last:
-                mm([(V(XL, 128, 256), V("id2"), B("ev"), True, False), (V(XL, 128, 256), V("idn"), B("xs"), False, True)])
-                act(V("win", w1 + OWN, w1 + OWN + M), V(XL, 128, 256), ACT.Identity, 1.0 - W)
-                send("S", t + 1, s, V("win", w1 + OWN, w1 + OWN + M), V("win", w1 + STR, w1 + STR + M))
-                mm([(V(XL, 256, 360), V("idp"), B("xs", LO - 1, M - 1), True, False), (V(XL, 256, 359), V("idn"), B("xs", LO, M - 1), False, True)])
+                ts(B("ev", LO, M), V(X, LO, M), M1, M1 + W // 2, A.add, A.subtract)
+                mm([(V(X, FX, FX + M), V("id2"), B("ev"), True, False), (V(X, FX, FX + M), V("idn"), B("xs"), False, True)])
+                mm([(V(X, DX, DX + 104), V("idp"), B("xs", LO - 1, M - 1), True, False), (V(X, DX, DX + 103), V("idn"), B("xs", LO, M - 1), False, True),
+                    (V(X, 0, 104), V("idp"), B("xs", LO, M), True, True)])
+                lin(ENG["fc"], V("em", e0 - EE + ES + 2 * EM, e0 - EE + ES + 2 * EM + M), V(X, FX, FX + M), 1.0, 1.0)
+                codes(t + 1, s)
+            else:
+                act(V(X, FX, FX + 104), V(X, LO, M), ACT.Identity, -0.25, -1.0)
             if ENG["pen"] == "v":
                 ts(B("pen"), B("xs", LO, M), 3000.0, None, A.is_gt)
             else:
                 act(B("pen"), B("xs", LO, M), ACT.Relu, -float(W // 2))
             mm([(V(K, 0, 104), V("idp"), V("low"), True, False), (V(K, 0, 104), V("idb"), B("pen"), False, False)])
-            for a, b, eng in CFG["FG"]:
+            for a, b, eng in CFG["FG"][s + (last and s)]:
                 gat(eng, B("R", 16 * a, 16 * b), V("bk", 0, W), B("ho", a, b))
-            TL, at = CFG["TL"], 0
+            TL = CFG["TL"][s + (last and s)]
             for ti, (mode, a, b) in enumerate(TL):
                 j0, j1, o, wd, fin = 16 * (a - LO), 16 * (b - LO), V(K, a - LO, b - LO), b - a, ti + 1 == len(TL)
                 if mode == "max":
@@ -286,21 +354,21 @@ def build():
             if last:
                 ts(B("sm", 7, 8), B("ai", t, t + 1), B("ai", 0, 1), None, A.subtract)
                 ts(B("sq"), V("idf"), B("sm", 7, 8), None, A.mult)
-                mm([(V(XL, 256, 360), B("sq"), V("one"), True, False)])
-                mm([(V(XL, 256, 360), sel("w1", cl), B("R", 16 + cl, 1680, 16), False, cl == 15) for cl in range(16)])
+                mm([(V(X, DX, DX + 104), B("sq"), V("one"), True, False)])
+                mm([(V(X, DX, DX + 104), sel("w1", cl), B("R", 16 + cl, 1680, 16), False, cl == 15) for cl in range(16)])
             red(B("sm", 0, 1), V(K, 0, 104), A.max, False, True)
             if ENG["mq"] == "v":
                 ts(B("mc"), V(K, 0, 104), B("sm", 0, 1), None, A.add)
             else:
                 act(B("mc"), V(K, 0, 104), ACT.Identity, B("sm", 0, 1))
             if not last:
-                scan(B("rr"), B("mc"), V(XL, 256, 360), -1e9, A.max)
+                scan(B("rr"), B("mc"), V(X, DX, DX + 104), -1e9, A.max)
                 scan(V("em", e0 + 2 * EM - 104, e0 + 2 * EM), B("mc"), V("cm"), -1e4, A.max)
                 ends(t + 1, s, B("rr", 103, 104))
             else:
                 scan(B("rr"), B("mc"), V("cz"), -1.0, A.max)
-                tt(V("yo", 2 * LO + s, 256, 2), V(XL, 128 + LO, 256), B("rr"), A.mult)
-                tt(B("pp", 0, 104), V(XL, 256, 360), B("mc"), A.add)
+                tt(V("yo", 2 * LO + s, 256, 2), V(X, FX, FX + 104), B("rr"), A.mult)
+                tt(B("pp", 0, 104), V(X, DX, DX + 104), B("mc"), A.add)
                 red(V("yb", s, s + 1), B("pp", 0, 104), A.max)
                 scan(V("yl", s, 208, 2), B("mc"), V("dl"), -1e4, A.max)
     add("s", "store", ("ys", V("yo")), [V("yo")], [], 60.0, 2200.0)
@@ -344,39 +412,49 @@ def link(ops):
 
 
 def order(ops, bias):
-    n = len(ops)
-    sem = CFG["sem"]
+    n, sem = len(ops), CFG["sem"]
+    fore = [[(j, ops[j]["lat"] + sem if w else 0.0) for j, w in o["deps"].items()] for o in ops]
+    back = [[(k, o["lat"] + sem if ops[k]["deps"][i] else 0.0) for k in o["succ"]] for i, o in enumerate(ops)]
+
+    def place(key, pre, post, least):
+        heap, left, busy, end, out = [(key[i], i) for i in range(n) if not pre[i]], [len(x) for x in pre], {}, [0.0] * n, []
+        while heap:
+            heap.sort()
+            i = heap.pop(0)[1]
+            at, cost = max([least[i]] + [end[j] + d for j, d in pre[i]]), ops[i]["cost"]
+            if ops[i]["eng"]:
+                lst = busy.setdefault(ops[i]["eng"], [])
+                p = len(lst)
+                while p and lst[p - 1][1] > at:
+                    p -= 1
+                while p < len(lst) and at + cost > lst[p][0]:
+                    at = max(at, lst[p][1])
+                    p += 1
+                lst.insert(p, (at, at + cost))
+            end[i] = at + cost
+            out.append(i)
+            for k, d in post[i]:
+                left[k] -= 1
+                if not left[k]:
+                    heap.append((key[k], k))
+        return end, out
+
     prio = [0.0] * n
     for i in range(n - 1, -1, -1):
-        prio[i] = ops[i]["cost"] + ops[i]["lat"] + max([prio[k] + (sem if ops[k]["deps"][i] else 0) for k in ops[i]["succ"]], default=0.0)
-    heap = [(-prio[i] - bias[i], i) for i in range(n) if not ops[i]["deps"]]
-    left = [len(o["deps"]) for o in ops]
-    busy, out, end, start = {}, [], [0.0] * n, [0.0] * n
-    while heap:
-        heap.sort()
-        i = heap.pop(0)[1]
-        o = ops[i]
-        at = max([end[j] + sem if w else end[j] if not o["eng"] else start[j] + ops[j]["cost"] for j, w in o["deps"].items()], default=0.0)
-        if o["eng"]:
-            lst = busy.setdefault(o["eng"], [])
-            p = len(lst)
-            while p and lst[p - 1][1] > at:
-                p -= 1
-            while p < len(lst) and at + o["cost"] > lst[p][0]:
-                at = max(at, lst[p][1])
-                p += 1
-            lst.insert(p, (at, at + o["cost"]))
-        start[i], end[i] = at, at + o["cost"] + o["lat"]
-        out.append(i)
-        for k in o["succ"]:
-            left[k] -= 1
-            if not left[k]:
-                heap.append((-prio[k] - bias[k], k))
-    pos = dict((i, p) for p, i in enumerate(out))
-    return sorted(out, key=lambda i: (start[i], pos[i])), start, end
+        prio[i] = ops[i]["cost"] + max([ops[i]["lat"]] + [prio[k] + d for k, d in back[i]])
+    key, best = [-prio[i] - bias[i] for i in range(n)], None
+    for it in range(CFG["turns"]):
+        end, out = place(key, fore, back, [0.0] * n)
+        last = max(end[i] + ops[i]["lat"] for i in range(n))
+        if best is None or last < best[0]:
+            pos = dict((i, p) for p, i in enumerate(out))
+            best = (last, sorted(out, key=lambda i: (end[i] - ops[i]["cost"], pos[i])))
+        if it + 1 < CFG["turns"]:
+            key = [-x for x in place([-x for x in end], back, fore, [o["lat"] for o in ops])[0]]
+    return best[1], best[0]
 
 
-def improve(ops, seq, cases):
+def improve(ops, bias, cases):
     n, ids, anc, wait, tags = len(ops), {}, [0] * len(ops), [], {}
     eng = [ids.setdefault(o["eng"] or i, len(ids)) for i, o in enumerate(ops)]
     for i, o in enumerate(ops):
@@ -429,16 +507,49 @@ def improve(ops, seq, cases):
                 rest.append(x)
         return seq[:p] + rest + take + seq[q + 1:] if k > 0 else seq[:q] + take[::-1] + rest[::-1] + seq[p + 1:]
 
-    rs, steps = np.random.RandomState(CFG["seed"]), CFG["steps"]
+    rs, steps, seq = np.random.RandomState(CFG["seed"]), CFG["steps"], order(ops, bias)[0]
     free = [i for i, o in enumerate(ops) if o["eng"] and o["kind"] != "load"]
     pick, ks = rs.randint(0, len(free), steps), rs.choice([-6, -3, -2, -1, -1, -1, 1, 1, 1, 2, 3, 6], steps)
     every, slack = rs.rand(steps) < 0.5, rs.exponential(size=steps) * CFG["temp"]
+    def queued(seq, case):
+        cost, lat, sem = case
+        f, who, r, why = [0.0] * len(ids), [-1] * len(ids), [0.0] * n, [(-1, False)] * n
+        for i in seq:
+            e, j = eng[i], arr[i]
+            a, why[i] = (r[j] - sem, (j, False)) if j >= 0 else (f[e], (who[e], True))
+            for j in wait[i]:
+                if r[j] > a:
+                    a, why[i] = r[j], (j, False)
+            f[e], who[e], r[i] = a + cost[i], i, a + cost[i] + lat[i] + sem
+        i, out = r.index(max(r)), []
+        while why[i][0] >= 0:
+            if why[i][1] and ops[why[i][0]]["kind"] != "load":
+                out += [(i, -1), (why[i][0], 1)]
+            i = why[i][0]
+        return out
+
+    now, names = replay(seq)[0], sorted(set(x for x in tags if isinstance(x, tuple)), key=lambda x: tags[x][0])
+    for it in range(CFG["tries"]):
+        at, wide, b2 = int(rs.randint(len(names))), int(rs.choice([1, 1, 2, 4, 8, 16])), list(bias)
+        amount = float(rs.normal()) * float(rs.choice([200.0, 600.0, 1500.0]))
+        for x in names[at:at + wide]:
+            for i in tags[x]:
+                b2[i] += amount
+        new = order(ops, b2)[0]
+        val = replay(new)[0]
+        if val <= now + CFG["warm"] * (1 - it / CFG["tries"]) * float(rs.exponential()):
+            now, bias, seq = val, b2, new
     now, ends = replay(seq)
     best = (now, ends, seq)
+    aim = rs.rand(steps) < CFG["aim"]
     for it in range(steps):
-        i, new = free[pick[it]], seq
+        if it % 16 == 0:
+            hot = queued(seq, cases[it // 16 % 3])
+        i, k, new = free[pick[it]], int(ks[it]), seq
+        if aim[it] and hot:
+            i, k = hot[pick[it] % len(hot)][0], hot[pick[it] % len(hot)][1] * abs(k)
         for x in (tags[ops[i].get("tag", i)] if every[it] else [i]):
-            new = move(new, new.index(x), int(ks[it])) or new
+            new = move(new, new.index(x), k) or new
         if new is not seq:
             val, ends = replay(new)
             if val <= now + slack[it] * (1 - it / steps):
@@ -462,10 +573,7 @@ def plan():
         ops = build()
         link(ops)
         bias = [-CFG["lag"] * o["s"] for o in ops]
-        for i, o in enumerate(ops):
-            if o["kind"] == "load":
-                bias[i] = 1e6 * (20 - i)
-        best = improve(ops, order(ops, bias)[0], cases)
+        best = improve(ops, bias, cases)
         PLAN.append((ops, best[2], best[1], cases))
     return PLAN[0]
 
@@ -489,6 +597,8 @@ def rank_program(g, core, T, topo):
     def ap(v):
         if not isinstance(v, tuple):
             return v
+        if len(v) > 4:
+            return T[v[0]][v[4]:v[5], v[1]:v[2]]
         return T[v[0]][:, v[1]:v[2]] if v[3] == 1 else T[v[0]][:, v[1]:v[2]:v[3]]
 
     ndma = 0

import numpy as np
from concourse.mybir import AluOpType, AxisListType, ActivationFunctionType

RO, M, LO, W, NR = 5, 128, 24, 4096, 8
CFG = {
    "SG": [[(0, 26, "a"), (26, 52, "v")],
           [(0, 30, "a"), (30, 42, "v"), (42, 52, "v")]],
    "RC": [[(0, 258, "a")], [(0, 258, "a")]],
    "FG": [[(0, 20, "v"), (20, 62, "a"), (62, 84, "v"), (84, 105, "v")], [(0, 20, "v"), (20, 62, "a"), (62, 84, "v"), (84, 94, "v"), (94, 105, "v")],
           [(0, 20, "v"), (20, 62, "a"), (62, 84, "v"), (84, 105, "v")]],
    "TL": [[("row", 24, 43), ("row", 43, 64), ("sum", 24, 64), ("row", 64, 85), ("row", 85, 107), ("row", 107, 128), ("sum", 64, 128)]] * 3,
    "eng": {"mq": "v", "pen": "v", "E": "v", "gr": "a", "dcl": 4, "hq": "v", "fc": "v", "gain": "a", "z": "v", "lin": "vvvaavvvaaav"}, "both": 1,
    "cyc": 0.9, "pe": 0.55, "gat": 1.4, "tt2": 2.0, "sem": 160.0, "issue": 600.0, "land": 2200.0, "fix": 90.0, "vfix": 50.0, "peu": 400,
    "first": 1200.0, "lag": 2000.0, "seed": 3, "steps": 50000, "temp": 300.0, "aim": 0.8, "turns": 1, "tries": 600, "warm": 600.0,
    "cases": [{"cyc": 0.83, "pe": 0.52, "gat": 1.15, "sem": 150.0, "fix": 70.0, "vfix": 40.0, "land": 1900.0, "issue": 400.0},
              {"cyc": 0.9, "pe": 0.5, "gat": 1.6, "sem": 110.0, "fix": 120.0, "vfix": 60.0, "land": 2300.0},
              {"cyc": 1.2, "pe": 0.75, "gat": 1.5, "sem": 170.0, "fix": 100.0, "vfix": 60.0, "land": 2800.0}],
}
REG, OWN, STR = 840, 168, 584
EM, EE, ES = 288, 112, 153
EL, LE, LS = 192, 8, 49
EB, FX, DX = 32, 232, 128
F32, BF, F16, I32, U16 = "float32", "bfloat16", "float16", "int32", "uint16"
SCRATCH = {}
for _n, _c, _d in (("bk", W + 16, BF), ("ar", 256, I32), ("ln", 4, I32), ("ti", 4, I32), ("win", REG * 2, F32), ("em", EM * 2 * RO, F16),
                   ("el", EL * 2 * RO, F16), ("thf", 2, F32), ("kk", 104, BF), ("iot", 144, BF), ("low", 104, BF), ("pmi", 128, BF),
                   ("blk", 128, BF), ("bm", 128, BF), ("pid", 4, I32), ("b8", 8, F32), ("pc", 12, F32), ("idp", 128, BF), ("idn", 128, BF), ("id2", 128, BF),
                   ("idb", 128, BF), ("idw", 128, BF), ("idf", 128, F32), ("tg", 128, F32), ("dn", 128, BF), ("dx", 104, F16),
                   ("Gx", 832, F16), ("xo", 104, F16), ("ofx", 52, U16), ("one", 104, F32), ("dcl", 2052, BF), ("wp", 144, BF), ("w2", 144, BF),
                   ("wn", 144, BF), ("w1", 144, BF), ("dg", 16, F32), ("fp", 16, F16), ("fn", 16, F16), ("od", 18, BF), ("cd", 18, F16),
                   ("cc", 128, BF), ("cq", 128, BF), ("cm", 104, BF), ("dl", 104, F32), ("cz", 104, F32), ("bo", 8, F32), ("rp", 260, BF),
                   ("onb", 128, BF), ("yo", 256, F32), ("yl", 208, F32), ("yb", 2, F32)):
    SCRATCH[_n] = ("sbuf", [128, _c], _d)
for _s in range(2):
    for _n, _c, _d in (("pp", 128, F32), ("sq", 128, F32), ("y0", 128, F32), ("xs", 128, F16), ("ev", 128, F16), ("mq", 128, F16),
                       ("mc", 104, F32), ("rr", 104, F32), ("si", 128, I32), ("hi", 128, I32), ("ho", 106, U16), ("R", 1680, BF),
                       ("AB", 1664, BF), ("G", 832, F16), ("xm", 128, F16), ("mz", 128, F16), ("off", 52, U16), ("pen", 104, BF),
                       ("nc", 104, F16), ("nz", 104, F16), ("yy", 52, F16), ("sm", 16, F32), ("ai", 8, F32), ("oq", 2, U16), ("orr", 2, U16), ("l8", 8, U16),
                       ("gq", 18, F32), ("gr", 16, BF)):
        SCRATCH["%s%d" % (_n, _s)] = ("sbuf", [128, _c], _d)
    SCRATCH["K%d" % _s] = ("psum", [128, 512], F32)
    SCRATCH["X%d" % _s] = ("psum", [128, 512], F32)
ND = 4
for _c in range(ND):
    SCRATCH["D%d" % _c] = ("psum", [128, 512], F32)
SEMAPHORES = (["cv", "ca", "cp", "cg", "sent"] + ["d%d" % i for i in range(10)]
              + ["a%s%d%d" % (k, t, s) for k in "SE" for t in range(RO) for s in range(2)])
A, ACT = AluOpType, ActivationFunctionType
M12, M1 = 1.5 * 2.0 ** 35, 1.5 * 2.0 ** 24
MARK, GAP = 4096.0, 8192.0


def V(name, lo=0, hi=None, step=1):
    return (name, lo, SCRATCH[name][1][1] if hi is None else hi, step)


def cols(v):
    return len(range(v[1], v[2], v[3]))


def build():
    ops, cur, sent = [], [0], []
    cyc, ENG = CFG["cyc"], CFG["eng"]

    def add(eng, kind, args, reads, writes, cost, lat=0.0, after=()):
        ops.append({"eng": eng, "kind": kind, "args": args, "r": [x for x in reads if isinstance(x, tuple)], "w": list(writes),
                    "cost": cost, "lat": lat, "after": list(after), "s": cur[0], "succ": []})
        if len(cur) > 1:
            key = (cur[0], eng, kind, (ops[-1]["w"] or ops[-1]["r"])[0][0])
            cur[1][key] = cur[1].get(key, 0) + 1
            ops[-1]["tag"] = key + (cur[1][key],)
        return len(ops) - 1

    def two(*vs):
        return all(SCRATCH[v[0]][2] in (BF, F16, U16) for v in vs)

    def vcost(n, f):
        return max(64, n * f) * cyc + CFG["vfix"]

    def ts(out, in0, s1, s2, op0, op1=None):
        add("v", "ts", (out, in0, s1, s2, op0, op1), [in0, s1, s2], [out], vcost(cols(out), 0.5 if two(out, in0) else 1))

    def tt(out, in0, in1, op):
        ps = SCRATCH[in0[0]][0] == "psum" or SCRATCH[in1[0]][0] == "psum"
        add("v", "tt", (out, in0, in1, op), [in0, in1], [out], vcost(cols(out), 1 if ps else CFG["tt2"] if two(out, in0, in1) else 2))

    def cp(out, in0):
        add("v", "cp", (out, in0), [in0], [out], vcost(cols(out), 0.5 if two(out, in0) else 1))

    def red(out, in0, op, ab=False, neg=False):
        add("v", "red", (out, in0, op, ab, neg), [in0], [out], vcost(cols(in0), 1))

    def fill(out, c):
        add("v", "fill", (out, c), [], [out], vcost(cols(out), 0.5 if two(out) else 1))

    def scan(out, d0, d1, ini, op):
        add("v", "scan", (out, d0, d1, ini, op), [d0, d1, ini], [out], vcost(cols(out), 1))

    def act(out, in0, func, bias=0.0, scale=1.0, acc=None):
        add("a", "act", (out, in0, func, bias, scale, acc), [in0, bias, scale], [out] + ([acc] if acc else []),
            CFG["fix"] + cols(out) * cyc + (20 if acc else 0))

    def gat(eng, out, win, off, mask=None):
        add(eng, "gat", (out, win, off, mask), [win, off, mask], [out], 60 + cols(out) * CFG["gat"] * cyc)

    def mm(lst):
        while lst:
            k, c = 0, 0
            while k < len(lst) and (c < CFG["peu"] or k % 2):
                k, c = k + 1, c + max(min(64, cols(lst[k][1])), cols(lst[k][2])) * (4 if SCRATCH[lst[k][2][0]][2] == F32 else 1)
            add("p", "mm", lst[:k], [x[1] for x in lst[:k]] + [x[2] for x in lst[:k]], [x[0] for x in lst[:k]], c * CFG["pe"], 60.0)
            lst = lst[k:]

    def iota(out, pattern, base, ch, after=()):
        add("g", "iota", (out, pattern, base, ch), [], [out], 130 + 2 * cols(out) * cyc, after=after)

    def const(out, c, after=()):
        iota(out, [[0, cols(out)]], int(c), 0, after)

    def lin(eng, out, in0, scale, bias):
        if eng == "v":
            ts(out, in0, scale, bias, A.mult, A.add)
        else:
            act(out, in0, ACT.Identity, bias, scale)

    def load(eng, out, name, lo, hi, lat):
        add(eng, "load", (out, name, lo, hi), [], [out], 60.0, lat, [i for i, o in enumerate(ops) if o["eng"] == eng])

    def send(kind, t, s, src, dst):
        sent.append(add("g", "send", (kind, t, s, src, dst), [src], [], CFG["issue"] + (0 if sent else CFG["first"]), after=sent[:1]))
        i = sent[-1]
        add(None, "arr", "a%s%d%d" % (kind, t, s), [], [dst], 0.0, CFG["land"] + 2 * cols(src), after=[i])

    load("s", V("ar"), "arms", 0, 256, 2200.0)
    load("a", V("ln", 0, 2), "len0", 0, 2, 2000.0)
    load("a", V("ti", 0, 2), "th", 0, 2, 2000.0)
    load("s", V("bk", 0, 2048), "bank", 0, 2048, 5000.0)
    load("a", V("bk", 2048, W), "bank", 2048, W, 5000.0)
    iota(V("pid", 0, 1), [[0, 1]], 0, 1)
    iota(V("iot"), [[1, 144]], 0, 0)
    iota(V("pmi"), [[1, 128]], 0, -1)
    iota(V("blk"), [[16, 8], [0, 16]], 0, 0)
    ts(V("pid", 1, 2), V("pid", 0, 1), 15, None, A.bitwise_and)
    CL, P16, P15, CLR = V("pc", 0, 1), V("pc", 1, 2), V("pc", 2, 3), V("pc", 3, 4)
    cp(CL, V("pid", 1, 2))
    ts(P16, V("pid", 0, 1), CL, None, A.subtract)
    ts(P15, P16, 15.0, None, A.add)
    ts(CLR, CL, 16.0 * (M - LO + 1), None, A.add)
    ts(V("dg"), V("iot", 0, 16), CL, None, A.is_equal)
    ts(V("bm"), V("blk"), P16, None, A.is_equal)
    ts(V("pid", 2, 3), V("pid", 0, 1), EB - 16, None, A.bitwise_and)
    cp(V("pc", 6, 7), V("pid", 2, 3))
    ts(V("b8"), V("iot", 0, 8), 16.0, V("pc", 6, 7), A.mult, A.is_equal)
    ts(V("bo"), V("b8"), -GAP, GAP + W // 2, A.mult, A.add)
    ts(V("fp"), V("iot", 0, 16), CL, None, A.is_equal)
    ts(V("od", 0, 16), V("iot", 0, 16), CL, -GAP, A.not_equal, A.mult)
    ts(V("idp"), V("pmi"), 0.0, None, A.is_equal)
    ts(V("wp"), V("iot"), P15, 128 * GAP, A.is_equal, A.mult)
    ts(V("pid", 3, 4), V("pid", 0, 1), 1, None, A.bitwise_and)
    ODD, EVEN, BASE = V("pc", 7, 8), V("pc", 8, 9), V("pc", 9, 10)
    cp(ODD, V("pid", 3, 4))
    lin("v", EVEN, ODD, -1.0, 1.0)
    lin("v", BASE, ODD, 1.0, float(OWN))
    for out, c in ((V("win", 0, REG * 2, REG), 0), (V("bk", W, W + 16), 0), (V("cm"), -2), (V("od", 16, 17), 0), (V("dcl", 0, 2), 0),
                   (V("dcl", 2050, 2052), 0), (V("rp", 0, 260, 130), 0), (V("rp", 129, 260, 130), 0)):
        const(out, c)
    for i in range(2):
        const(V("win", REG * i + 8, REG * i + OWN - 2), MARK)
        const(V("win", REG * i + OWN + 2 * M, REG * i + STR - 2), MARK)
    for c, x in ((ES - 1, MARK), (ES + M, 0.0), (EE - 2, 0.0), (ES - 3, 0.0)):
        lin("v", V("em", c, EM * 2 * RO, EM), V("iot", 0, 2 * RO), 0.0, x)
    lin("a", V("cd", 0, 16), V("iot", 0, 16), 0.0, 0.0)
    lin("a", V("cd", 16, 17), BASE, 1.0, 2.0 * M)
    lin("a", V("cd", 17, 18), BASE, 0.0, float(STR - OWN))
    lin("v", V("rp", 1, 129), V("idp"), EVEN, 0.0)
    lin("v", V("rp", 131, 259), V("idp"), ODD, 0.0)
    e = iter(ENG["lin"])
    lin(next(e), V("pc", 4, 5), V("dg", 0, 1), W / 2, 0.0)
    lin(next(e), V("pc", 5, 6), V("dg", 1, 2), -0.25, V("pc", 4, 5))
    lin(next(e), V("cc"), V("iot", 0, 128), 0.0, V("pc", 5, 6))
    lin(next(e), V("cq"), V("iot", 0, 128), 0.0, 0.25)
    lin(next(e), V("low"), V("iot", LO, M), -GAP, 0.0)
    lin(next(e), V("kk"), V("iot", LO, M), 2.0, -2.0 * M)
    lin(next(e), V("fn"), V("fp"), -1.0, 0.0)
    for name, c in (("idn", -1.0), ("id2", 2.0), ("idw", -float(W)), ("idb", -2.0 ** (33 if ENG["pen"] == "v" else 22)), ("idf", 1.0)):
        lin(next(e), V(name), V("idp"), c, 0.0)
    for name, c in (("w1", 2.0 ** -20), ("w2", 2.0), ("wn", -1.0)):
        if name == "w1" or any(x[0] == "max" for y in CFG["TL"] for x in y):
            lin("a", V(name), V("wp"), c, 0.0)
    for cl in range(16):
        lin("v" if cl < ENG["dcl"] else "a", V("dcl", 128 * cl + 2, 128 * cl + 130), V("idp"), V("dg", cl, cl + 1), 0.0)
    cp(V("thf"), V("ti", 0, 2))

    def ends(t, s, code):
        e0, l0 = EM * (2 * t + s) + EE, EL * (2 * t + s) + LE
        ts(V("l8%d" % s, 0, EB // 16), V("bo", 0, EB // 16), code, float(W), A.add, A.min)
        gat(ENG["E"], V("em", e0, e0 + EB), V("bk"), V("l8%d" % s, 0, EB // 16))
        send("E", t, s, V("em", e0 - 2, e0 + EB), V("el", l0 - 2, l0 + EB))

    def codes(t, s):
        c0, l0, more = EM * (2 * t + s) + ES, EL * (2 * t + s) + LS, 1 if t else 3
        send("S", t, s, V("em", c0 - more, c0 + M + 1), V("el", l0 - more, l0 + M + 1))

    def lanes(s, name, c0, who):
        X, w0 = "X%d" % s, REG * s + (OWN, STR)[who] - 2
        mm([(V(X, FX + ch, FX + 258, 2), V("rp", 130 * ch + 1 + ch - i, 130 * ch + 129 + ch - i), V(name, c0 - i, c0 - i + M + 1), i == 0, i == 1)
            for ch in range(2) for i in range(2)])
        for a, b, eng in CFG["RC"][who]:
            if eng == "a":
                act(V("win", w0 + a, w0 + b), V(X, FX + a, FX + b), ACT.Copy)
            else:
                cp(V("win", w0 + a, w0 + b), V(X, FX + a, FX + b))

    def diagonal(out, G, i, alone):
        mm([(out, V("dcl", 128 * (c // 2 * 2 + i) + 2 + i - c % 2, 128 * (c // 2 * 2 + i) + 130 + i - c % 2), V(G, c, 832, 16),
             alone and c == 0, alone and c == 15) for c in range(16)])

    def turn(out, src, pick, stop):
        return [(out + (p, p + EB), src + (p, p + EB), pick + (p, p + EB), False, stop) for p in range(0, 128, EB)]

    for s in range(2):
        B = lambda n, lo=0, hi=None, st=1: V("%s%d" % (n, s), lo, hi, st)
        cur[0] = s
        n_ = B("sm", 8, 9)
        ts(B("xs"), V("ar", s, 256, 2), -float(W // 2), None, A.add)
        ts(B("si"), V("ar", s, 256, 2), W - 2, None, A.bitwise_and)
        ts(B("X", 0, M), B("si"), 2.0, 1.0 - W, A.mult, A.add)
        tt(V("em", EM * s + ES, EM * s + ES + M), B("X", 0, M), B("xs"), A.subtract)
        act(B("y0"), B("xs"), ACT.Copy)
        for out in (V("em", EM * s + ES - 2, EM * s + ES - 1), n_, V("em", EM * s + EE - 1, EM * s + EE)):
            ts(out, V("ln", s, s + 1), 2.0, -2.0 * M, A.mult, A.add)
        codes(0, s)
        ts(B("oq", 0, 1), V("ln", s, s + 1), -1.0, None, A.add)
        gat("v", B("gq", 0, 16), B("y0"), B("oq", 0, 1), V("dg"))
        red(B("sm", 2, 3), B("gq", 0, 16), A.add)
        ends(0, s, B("sm", 2, 3))
        act(B("ev", 0, LO), B("X", 0, LO), ACT.Identity, -0.5, 0.5)
        act(B("xm", LO - 1, LO), B("xs", LO - 1, LO), ACT.Copy)
        act(B("sq", 0, LO - 1), B("xs", 0, LO - 1), ACT.Copy, acc=B("sm", 6, 7))
        act(B("ai", 0, 1), B("sm", 6, 7), ACT.Identity, (LO - 1) * (W // 2) + 2048.5)
        act(V("yo", s, 2 * LO, 2), B("xs", 0, LO), ACT.Identity, W / 2)
        ts(B("pen"), V("kk"), n_, -GAP, A.not_equal, A.mult)
        scan(B("nc"), B("pen"), V("cm"), -1e4, A.max)
    for out, c in ((V("one"), 1), (V("cz"), 0), (V("dl", 0, 103), -1), (V("dl", 103, 104), M - 1)):
        const(out, c, sent[-1:])

    tile = [0]
    for t in range(RO):
        for s in range(2):
            B = lambda n, lo=0, hi=None, st=1: V("%s%d" % (n, s), lo, hi, st)
            e0, l0, w0 = EM * (2 * t + s) + EE, EL * (2 * t + s) + LE, REG * s
            n_, n2 = V("em", e0 - 1, e0), V("el", l0 - 1, l0)
            nc = V("em", e0 - 104, e0) if t else B("nc")
            odd, even = (nc[0], nc[1] + 1, nc[2], 2), (nc[0], nc[1], nc[2], 2)
            K, X, last = "K%d" % s, "X%d" % s, t + 1 == RO
            both = t == 0 and s < CFG["both"]
            cur[:] = [s, {}]
            sel = lambda n, cl: V(n, 15 - cl, 143 - cl)
            ts(B("mz", LO, M), nc, -1000.0, None, A.is_lt)
            tt(B("xm", LO, M), V(X, 0, 104) if t else B("xs", LO, M), B("mz", LO, M), A.mult)
            lanes(s, "em", e0 - EE + ES, 0)
            lanes(s, "el", l0 - LE + LS, 1)
            if t:
                ts(B("orr", 0, 1), n_, 8.0, CLR, A.mult, A.add)
                gat(ENG["gr"], B("gr"), B("R"), B("orr", 0, 1))
                if ENG["gain"] == "p":
                    mm([(V(K, 104, 121), V("idp"), V("od", 0, 17), True, False), (V(K, 120, 121), V("idf"), B("ai", t - 1, t), False, False),
                        (V(K, 104, 120), V("bm"), B("gr"), False, True)])
                    act(B("gq", 0, 17), V(K, 104, 121), ACT.Relu, acc=B("ai", t, t + 1))
                else:
                    mm([(V(K, 104, 120), V("idp"), V("od", 0, 16), True, False), (V(K, 104, 120), V("bm"), B("gr"), False, True)])
                    red(B("sm", 11, 12), V(K, 104, 120), A.max)
                    lin(ENG["gain"], B("ai", t, t + 1), B("sm", 11, 12), 1.0, B("ai", t - 1, t))
            mm([(V(K, 128, 146), V("idp"), V("cd"), True, False), (V(K, 144, 145), V("idp"), n_, False, False),
                (V(K, 145, 146), V("idn"), n_, False, False)] + turn(V(K, 128, 144), V("em", e0, e0 + EB), V("fp"), False))
            mm([(V(K, 145, 146), V("idp"), n2, False, False)] + turn(V(K, 128, 144), V("el", l0, l0 + EB), V("fn"), True))
            red(B("sm", 3, 4), V(K, 128, 144), A.add, True)
            if both:
                ts(B("sm", 9, 10), B("sm", 8, 9), BASE, 2.0 * M, A.add, A.add)
                ts(B("sm", 10, 11), V("el", l0 - LE + LS - 2, l0 - LE + LS - 1), BASE, 2.0 * M + STR - OWN, A.add, A.add)
                for G, off, end, D, at in (("Gx", "ofx", STR - 2, "D0", 9), (B("G")[0], B("off")[0], REG, "D1", 10)):
                    ts(V(off), odd, B("sm", at, at + 1), None, A.add)
                    for a, b, eng in CFG["SG"][s]:
                        gat(eng, V(G, 16 * a, 16 * b), V("win", w0, w0 + end), V(off, a, b))
                    for i in range(2):
                        diagonal(V(D, i, 104, 2), G, i, True)
                ts(B("nz"), nc, -1000.0, -1.0, A.is_gt, A.mult)
                tt(V("xo"), V("D0", 0, 104), B("nz"), A.mult)
                ts(B("nz"), nc, -1000.0, None, A.is_gt)
                tt(V("dx"), V("D1", 0, 104), B("nz"), A.mult)
                ts(V("tg"), V("idf"), V("thf", s, s + 1), None, A.mult)
                ts(V("dn"), V("tg"), B("sm", 3, 4), None, A.is_gt)
            else:
                ts(B("sm", 5, 6), B("sm", 3, 4), V("thf", s, s + 1), V(K, 145, 146), A.is_lt, A.mult)
                ts(B("off"), odd, B("sm", 5, 6), V(K, 144, 145), A.add, A.add)
                for a, b, eng in CFG["SG"][s]:
                    gat(eng, B("G", 16 * a, 16 * b), V("win", w0, w0 + REG), B("off", a, b))
            lo, hi = LO - 1, M
            mm([(V(X, lo, hi), V("bm"), V("cc", lo, hi), True, False), (V(X, lo, hi), V("idp"), B("xm", lo, hi), False, False)])
            if both:
                mm([(V(X, LO, M), V("idn"), V("xo"), False, False)])
                mm([(V(X, LO, M), V("dn"), V("xo"), False, False), (V(X, LO, M), V("dn"), V("dx"), False, True)])
            else:
                ts(B("nz", 0, 52), even, -1000.0, None, A.is_gt)
                diagonal(V(K, 300, 352), B("G")[0], 0, True)
                diagonal(V(X, LO + 1, M, 2), B("G")[0], 1, False)
                tt(B("yy"), V(K, 300, 352), B("nz", 0, 52), A.mult)
                mm([(V(X, LO, M, 2), V("idp"), B("yy"), False, True)])
            Z = V(K, 160 + lo, 160 + hi)
            scan(B("pp", lo, hi), V("cq", lo, hi), V(X, lo, hi), B("ai", t, t + 1), A.add)
            act(B("xs", LO, M), V(X, LO, M), ACT.Identity, -2047.75)
            if ENG["z"] == "p":
                lin(ENG["hq"], B("mq", lo, hi), B("pp", lo, hi), 1.0 / W, 1024.0)
                mm([(Z, V("idf"), B("pp", lo, hi), True, False)])
                mm([(Z, V("idw"), B("mq", lo, hi), False, True)])
                act(B("sq", lo, hi), Z, ACT.Square, 511.875 + 2.0 ** 20, 0.25)
            else:
                ts(Z, B("pp", lo, hi), M12, M12, A.add, A.subtract)
                tt(B("y0", lo, hi), B("pp", lo, hi), Z, A.subtract)
                act(B("sq", lo, hi), B("y0", lo, hi), ACT.Square, 511.875, 0.25)
            tt(B("si", lo, hi), V(X, lo, hi), B("sq", lo, hi), A.add)
            ts(B("hi", lo, hi), B("si", lo, hi), W - 1, None, A.bitwise_and)
            cp(B("ho", 0, hi - lo), B("hi", lo, hi))
            if not last:
                ts(B("ev", LO, M), V(X, LO, M), M1, M1 + W // 2, A.add, A.subtract)
                mm([(V(X, FX, FX + M), V("id2"), B("ev"), True, False), (V(X, FX, FX + M), V("idn"), B("xs"), False, True)])
                mm([(V(X, DX, DX + 104), V("idp"), B("xs", LO - 1, M - 1), True, False), (V(X, DX, DX + 103), V("idn"), B("xs", LO, M - 1), False, True),
                    (V(X, 0, 104), V("idp"), B("xs", LO, M), True, True)])
                lin(ENG["fc"], V("em", e0 - EE + ES + 2 * EM, e0 - EE + ES + 2 * EM + M), V(X, FX, FX + M), 1.0, 1.0)
                codes(t + 1, s)
            else:
                act(V(X, FX, FX + 104), V(X, LO, M), ACT.Identity, -0.25, -1.0)
            if ENG["pen"] == "v":
                ts(B("pen"), B("xs", LO, M), 3000.0, None, A.is_gt)
            else:
                act(B("pen"), B("xs", LO, M), ACT.Relu, -float(W // 2))
            mm([(V(K, 0, 104), V("idp"), V("low"), True, False), (V(K, 0, 104), V("idb"), B("pen"), False, False)])
            for a, b, eng in CFG["FG"][s + (last and s)]:
                gat(eng, B("R", 16 * a, 16 * b), V("bk", 0, W), B("ho", a, b))
            TL = CFG["TL"][s + (last and s)]
            for ti, (mode, a, b) in enumerate(TL):
                j0, j1, o, wd, fin = 16 * (a - LO), 16 * (b - LO), V(K, a - LO, b - LO), b - a, ti + 1 == len(TL)
                if mode == "max":
                    tt(B("AB", j0, j1), B("R", j0 + 16, j1 + 16), B("R", j0, j1), A.max)
                    mm([(o, sel("wn", cl), B("R", j0 + u + cl, j1 + u, 16), False, False) for cl in range(16) for u in (0, 16)])
                    mm([(o, sel("w2", cl), B("AB", j0 + cl, j1, 16), False, fin and cl == 15) for cl in range(16)])
                elif mode == "row":
                    D = "D%d" % (tile[0] % ND)
                    tile[0] += 1
                    mm([(V(D, 0, j1 - j0), V("idp"), B("R", j0 + 16, j1 + 16), True, False), (V(D, 0, j1 - j0), V("idn"), B("R", j0, j1), False, True)])
                    act(B("AB", j0, j1), V(D, 0, j1 - j0), ACT.Abs)
                else:
                    mm([(o, sel("wp", cl), B("AB", j0 + cl, j1, 16), False, fin and cl == 15) for cl in range(16)])
            if last:
                ts(B("sm", 7, 8), B("ai", t, t + 1), B("ai", 0, 1), None, A.subtract)
                ts(B("sq"), V("idf"), B("sm", 7, 8), None, A.mult)
                mm([(V(X, DX, DX + 104), B("sq"), V("one"), True, False)])
                mm([(V(X, DX, DX + 104), sel("w1", cl), B("R", 16 + cl, 1680, 16), False, cl == 15) for cl in range(16)])
            red(B("sm", 0, 1), V(K, 0, 104), A.max, False, True)
            if ENG["mq"] == "v":
                ts(B("mc"), V(K, 0, 104), B("sm", 0, 1), None, A.add)
            else:
                act(B("mc"), V(K, 0, 104), ACT.Identity, B("sm", 0, 1))
            if not last:
                scan(B("rr"), B("mc"), V(X, DX, DX + 104), -1e9, A.max)
                scan(V("em", e0 + 2 * EM - 104, e0 + 2 * EM), B("mc"), V("cm"), -1e4, A.max)
                ends(t + 1, s, B("rr", 103, 104))
            else:
                scan(B("rr"), B("mc"), V("cz"), -1.0, A.max)
                tt(V("yo", 2 * LO + s, 256, 2), V(X, FX, FX + 104), B("rr"), A.mult)
                tt(B("pp", 0, 104), V(X, DX, DX + 104), B("mc"), A.add)
                red(V("yb", s, s + 1), B("pp", 0, 104), A.max)
                scan(V("yl", s, 208, 2), B("mc"), V("dl"), -1e4, A.max)
    add("s", "store", ("ys", V("yo")), [V("yo")], [], 60.0, 2200.0)
    add("s", "store", ("yn", V("yl", 206, 208)), [V("yl")], [], 60.0, 2000.0)
    add("a", "store", ("ya", V("yb")), [V("yb")], [], 60.0, 2000.0)
    return ops


def link(ops):
    hist = {}
    for i, o in enumerate(ops):
        deps = dict((j, False) for j in o["after"])
        acc = [(v, False) for v in o["r"]] + [(v, True) for v in o["w"]]
        for v, wr in acc:
            ps = SCRATCH[v[0]][0] == "psum"
            for j, lo, hi, w in hist.get(v[0], ()):
                same = ops[j]["eng"] == o["eng"] and ops[j]["kind"] not in ("load", "send") and o["kind"] not in ("store", "send")
                hit = lo < v[2] and v[1] < hi
                if ps:
                    need = (not same) or (hit and (w or wr))
                    if same and not need and o["eng"] != "p":
                        continue
                elif hit and (w or wr):
                    need = True
                else:
                    continue
                if o["eng"] == "p" and same:
                    need = False
                deps[j] = deps.get(j, False) or need
        o["deps"] = deps
        for j in deps:
            ops[j]["succ"].append(i)
        for v, wr in acc:
            h = hist.setdefault(v[0], [])
            if SCRATCH[v[0]][0] == "psum":
                h[:] = [x for x in h[-24:] if x[0] != i or (x[3] and not wr)]
                v = (v[0], 0, 512) if o["eng"] == "p" else v
            elif wr and v[3] == 1:
                h[:] = [x for x in h if not (v[1] <= x[1] and x[2] <= v[2])]
            h.append((i, v[1], v[2], wr))


def order(ops, bias):
    n, sem = len(ops), CFG["sem"]
    fore = [[(j, ops[j]["lat"] + sem if w else 0.0) for j, w in o["deps"].items()] for o in ops]
    back = [[(k, o["lat"] + sem if ops[k]["deps"][i] else 0.0) for k in o["succ"]] for i, o in enumerate(ops)]

    def place(key, pre, post, least):
        heap, left, busy, end, out = [(key[i], i) for i in range(n) if not pre[i]], [len(x) for x in pre], {}, [0.0] * n, []
        while heap:
            heap.sort()
            i = heap.pop(0)[1]
            at, cost = max([least[i]] + [end[j] + d for j, d in pre[i]]), ops[i]["cost"]
            if ops[i]["eng"]:
                lst = busy.setdefault(ops[i]["eng"], [])
                p = len(lst)
                while p and lst[p - 1][1] > at:
                    p -= 1
                while p < len(lst) and at + cost > lst[p][0]:
                    at = max(at, lst[p][1])
                    p += 1
                lst.insert(p, (at, at + cost))
            end[i] = at + cost
            out.append(i)
            for k, d in post[i]:
                left[k] -= 1
                if not left[k]:
                    heap.append((key[k], k))
        return end, out

    prio = [0.0] * n
    for i in range(n - 1, -1, -1):
        prio[i] = ops[i]["cost"] + max([ops[i]["lat"]] + [prio[k] + d for k, d in back[i]])
    key, best = [-prio[i] - bias[i] for i in range(n)], None
    for it in range(CFG["turns"]):
        end, out = place(key, fore, back, [0.0] * n)
        last = max(end[i] + ops[i]["lat"] for i in range(n))
        if best is None or last < best[0]:
            pos = dict((i, p) for p, i in enumerate(out))
            best = (last, sorted(out, key=lambda i: (end[i] - ops[i]["cost"], pos[i])))
        if it + 1 < CFG["turns"]:
            key = [-x for x in place([-x for x in end], back, fore, [o["lat"] for o in ops])[0]]
    return best[1], best[0]


def improve(ops, bias, cases):
    n, ids, anc, wait, tags = len(ops), {}, [0] * len(ops), [], {}
    eng = [ids.setdefault(o["eng"] or i, len(ids)) for i, o in enumerate(ops)]
    for i, o in enumerate(ops):
        keep = []
        for j in sorted([j for j, w in o["deps"].items() if w], reverse=True):
            if not anc[i] >> j & 1:
                keep.append(j)
                anc[i] |= anc[j] | 1 << j
        wait.append(keep)
        tags.setdefault(o.get("tag", i), []).append(i)
    deps, succ = [list(o["deps"]) for o in ops], [o["succ"] for o in ops]
    arr = [-1 if o["eng"] else o["after"][0] for o in ops]
    (c0, l0, s0), (c1, l1, s1), (c2, l2, s2) = cases
    r0, r1, r2 = [0.0] * n, [0.0] * n, [0.0] * n

    def replay(seq):
        f0, f1, f2 = [0.0] * len(ids), [0.0] * len(ids), [0.0] * len(ids)
        for i in seq:
            e, j = eng[i], arr[i]
            a0, a1, a2 = (r0[j] - s0, r1[j] - s1, r2[j] - s2) if j >= 0 else (f0[e], f1[e], f2[e])
            for j in wait[i]:
                if r0[j] > a0:
                    a0 = r0[j]
                if r1[j] > a1:
                    a1 = r1[j]
                if r2[j] > a2:
                    a2 = r2[j]
            f0[e], f1[e], f2[e] = a0 + c0[i], a1 + c1[i], a2 + c2[i]
            r0[i], r1[i], r2[i] = f0[e] + l0[i] + s0, f1[e] + l1[i] + s1, f2[e] + l2[i] + s2
        ends = (max(r0), max(r1), max(r2))
        return ends[0] + ends[1] + 0.8 * ends[2] + 0.5 * (sum(r0) + sum(r1) + 0.8 * sum(r2)) / n, ends

    def move(seq, p, k):
        i, q, left = seq[p], p, abs(k)
        while left:
            q += 1 if k > 0 else -1
            if not 0 <= q < n:
                return None
            left -= eng[seq[q]] == eng[i]
        rel = succ if k > 0 else deps
        need, engs, take, rest = set(rel[i]), set(), [i], []
        for x in (seq[p + 1:q + 1] if k > 0 else seq[q:p][::-1]):
            if x in need or eng[x] in engs:
                if eng[x] == eng[i]:
                    return None
                take.append(x)
                need.update(rel[x])
                engs.add(eng[x])
            else:
                rest.append(x)
        return seq[:p] + rest + take + seq[q + 1:] if k > 0 else seq[:q] + take[::-1] + rest[::-1] + seq[p + 1:]

    rs, steps, seq = np.random.RandomState(CFG["seed"]), CFG["steps"], order(ops, bias)[0]
    free = [i for i, o in enumerate(ops) if o["eng"] and o["kind"] != "load"]
    pick, ks = rs.randint(0, len(free), steps), rs.choice([-6, -3, -2, -1, -1, -1, 1, 1, 1, 2, 3, 6], steps)
    every, slack = rs.rand(steps) < 0.5, rs.exponential(size=steps) * CFG["temp"]
    def queued(seq, case):
        cost, lat, sem = case
        f, who, r, why = [0.0] * len(ids), [-1] * len(ids), [0.0] * n, [(-1, False)] * n
        for i in seq:
            e, j = eng[i], arr[i]
            a, why[i] = (r[j] - sem, (j, False)) if j >= 0 else (f[e], (who[e], True))
            for j in wait[i]:
                if r[j] > a:
                    a, why[i] = r[j], (j, False)
            f[e], who[e], r[i] = a + cost[i], i, a + cost[i] + lat[i] + sem
        i, out = r.index(max(r)), []
        while why[i][0] >= 0:
            if why[i][1] and ops[why[i][0]]["kind"] != "load":
                out += [(i, -1), (why[i][0], 1)]
            i = why[i][0]
        return out

    now, names = replay(seq)[0], sorted(set(x for x in tags if isinstance(x, tuple)), key=lambda x: tags[x][0])
    for it in range(CFG["tries"]):
        at, wide, b2 = int(rs.randint(len(names))), int(rs.choice([1, 1, 2, 4, 8, 16])), list(bias)
        amount = float(rs.normal()) * float(rs.choice([200.0, 600.0, 1500.0]))
        for x in names[at:at + wide]:
            for i in tags[x]:
                b2[i] += amount
        new = order(ops, b2)[0]
        val = replay(new)[0]
        if val <= now + CFG["warm"] * (1 - it / CFG["tries"]) * float(rs.exponential()):
            now, bias, seq = val, b2, new
    now, ends = replay(seq)
    best = (now, ends, seq)
    aim = rs.rand(steps) < CFG["aim"]
    for it in range(steps):
        if it % 16 == 0:
            hot = queued(seq, cases[it // 16 % 3])
        i, k, new = free[pick[it]], int(ks[it]), seq
        if aim[it] and hot:
            i, k = hot[pick[it] % len(hot)][0], hot[pick[it] % len(hot)][1] * abs(k)
        for x in (tags[ops[i].get("tag", i)] if every[it] else [i]):
            new = move(new, new.index(x), k) or new
        if new is not seq:
            val, ends = replay(new)
            if val <= now + slack[it] * (1 - it / steps):
                now, seq = val, new
                if val < best[0]:
                    best = (val, ends, new)
    return best


PLAN = []


def plan():
    if not PLAN:
        cases, keep = [], dict(CFG)
        for c in CFG["cases"]:
            CFG.update(c)
            ops = build()
            cases.append(([o["cost"] for o in ops], [o["lat"] for o in ops], CFG["sem"]))
            CFG.update(keep)
        ops = build()
        link(ops)
        bias = [-CFG["lag"] * o["s"] for o in ops]
        best = improve(ops, bias, cases)
        PLAN.append((ops, best[2], best[1], cases))
    return PLAN[0]


def rank_program(g, core, T, topo):
    rank = T.rank_of(core)
    if rank is None:
        return
    ops, seq = plan()[:2]
    peers = [T.cores[(rank + 1 + t % (NR - 1)) % NR] for t in range(RO)]
    mask = -1
    for a in T.cores:
        for b in T.cores:
            if a != b:
                mask &= topo.mask(a, b)
    lanes = bin(mask).count("1")
    queue = {"v": g.vector, "a": g.scalar, "p": g.tensor, "g": g, "s": g.sync}
    csem = {"v": "cv", "a": "ca", "p": "cp", "g": "cg"}
    total, known, mark, clock = {}, dict((e, {}) for e in queue), {}, {}

    def ap(v):
        if not isinstance(v, tuple):
            return v
        if len(v) > 4:
            return T[v[0]][v[4]:v[5], v[1]:v[2]]
        return T[v[0]][:, v[1]:v[2]] if v[3] == 1 else T[v[0]][:, v[1]:v[2]:v[3]]

    ndma = 0
    for i in seq:
        o = ops[i]
        e, kind, x = o["eng"], o["kind"], o["args"]
        if kind == "arr":
            mark[i], clock[i], total[x] = (x, lanes), {}, lanes
            continue
        q, kn = queue[e], known[e]
        need = sorted([j for j, w in o["deps"].items() if w and j in mark], key=lambda j: -mark[j][1])
        for j in need:
            sname, cnt = mark[j]
            if kn.get(sname, 0) < cnt:
                q.wait_ge(T.sem[sname], cnt)
                kn[sname] = cnt
                for k2, c2 in clock[j].items():
                    kn[k2] = max(kn.get(k2, 0), c2)
        clock[i] = dict(kn)
        if kind == "send":
            rid, pid = topo.addr(peers[x[1]])[:2]
            g.remote_dma(ap(x[4]), ap(x[3]), T.sem["a%s%d%d" % x[:3]], T.sem.sent, pid, rid, mask)
            total["sent"] = total.get("sent", 0) + lanes
            continue
        if kind in ("load", "store"):
            sname = "d%d" % ndma
            ndma += 1
            ins = q.dma_start(ap(x[0]), T[x[1]][:, x[2]:x[3]]) if kind == "load" else q.dma_start(T[x[0]][:], ap(x[1]))
            ins.then_inc(T.sem[sname], 16)
            mark[i], total[sname] = (sname, 16), 16
            continue
        if kind == "ts":
            ins = (q.tensor_scalar(ap(x[0]), ap(x[1]), ap(x[2]), None, x[4]) if x[5] is None
                   else q.tensor_scalar(ap(x[0]), ap(x[1]), ap(x[2]), ap(x[3]), x[4], x[5]))
        elif kind == "tt":
            ins = q.tensor_tensor(ap(x[0]), ap(x[1]), ap(x[2]), x[3])
        elif kind == "cp":
            ins = q.tensor_copy(ap(x[0]), ap(x[1]))
        elif kind == "red":
            ins = q.tensor_reduce(ap(x[0]), ap(x[1]), AxisListType.X, x[2], negate=x[4], apply_absolute_value=x[3])
        elif kind == "fill":
            ins = q.memset(ap(x[0]), x[1])
        elif kind == "scan":
            ins = q.tensor_tensor_scan(ap(x[0]), ap(x[1]), ap(x[2]), ap(x[3]), x[4], A.add)
        elif kind == "act":
            ins = q.activation(ap(x[0]), ap(x[1]), x[2], bias=ap(x[3]), scale=ap(x[4]), accum_out=ap(x[5]))
        elif kind == "gat":
            src = ap(x[1]).indirect(ap(x[2]))
            if e == "a":
                ins = q.activation(ap(x[0]), src, ACT.Copy)
            elif x[3] is None:
                ins = q.tensor_copy(ap(x[0]), src)
            else:
                ins = q.tensor_tensor(ap(x[0]), src, ap(x[3]), A.mult)
        elif kind == "iota":
            if SCRATCH[x[0][0]][2] == I32:
                ins = q.iota(ap(x[0]), x[1], x[2], x[3])
            else:
                ins = q.iota(ap(x[0]), x[1], x[2], x[3], allow_small_or_imprecise_dtypes=True)
        else:
            for mo, ml, mr, st, sp in x:
                ins = q.matmul(ap(mo), ap(ml), ap(mr), st, sp)
        sname = csem[e]
        total[sname] = total.get(sname, 0) + 1
        ins.then_inc(T.sem[sname], 1)
        mark[i] = (sname, total[sname])
    for sname, cnt in total.items():
        if known["s"].get(sname, 0) < cnt:
            g.sync.wait_ge(T.sem[sname], cnt)
